import numpy as np, ml_dtypes
CORES = [16,17,18,19,32,33,34,35]
N = 8
import mx_ref
BF = ml_dtypes.bfloat16
def gcols(t, e):
    v = np.concatenate([t.reshape(8, 16, -1, 4), np.zeros((8, 16, 1, 4), BF)], axis=2)
    return np.ascontiguousarray(np.stack([v[g][:, e[g]] for g in range(8)])).reshape(128, -1)
def cut(t, i, w=512):
    return t[:, w * i:w * i + w]
def pick(q, e):
    c = np.concatenate([q[0].reshape(128, -1, 4), np.zeros((128, 1, 4), np.uint8)], axis=1); s = np.concatenate([q[1], np.ones((16, 1), np.uint8)], axis=1)
    return (np.ascontiguousarray(c[:, e].reshape(128, -1)), np.ascontiguousarray(s[:, e]))
def join(*qs):
    return (np.concatenate([q[0] for q in qs], axis=1), np.concatenate([q[1] for q in qs], axis=1))
def put(q, e, v):
    c, s = q[0].reshape(128, -1, 4).copy(), q[1].copy(); c[:, e] = v[0].reshape(128, -1, 4); s[:, e] = v[1]
    return (c.reshape(128, -1), s)
def pk(c, s):
    return (np.ascontiguousarray(c), mx_ref.live(s))
def emit(q):
    return q[0], q[1]
def packed(v, rng):
    q = [mx_ref.quantize(np.ascontiguousarray(v[r])) for r in range(N)]
    return np.stack([a for a, b in q]), np.stack([mx_ref.plane(b, rng) for a, b in q])
def values_of_codes():
    e, c = np.zeros((128, 128, 4), np.float32), np.zeros((128, 2, 4), np.uint8)
    e[np.arange(128), np.arange(128), 0] = 1
    c[:127, :, 0] = np.arange(256).reshape(2, 128).T[:127]
    return mx_ref.matmul(mx_ref.quantize(e.reshape(128, 512).astype(BF)), (c.reshape(128, 8), np.full((16, 2), 127, np.uint8))).T.reshape(-1).astype(np.float64)
CODE_VALUE, SCALE_VALUE = values_of_codes(), 2.0 ** (np.arange(256) - 127.0)
def decode(q):
    return (CODE_VALUE[q[0]].reshape(16, 8, -1, 4) * SCALE_VALUE[q[1]][:, None, :, None] + 0.0).reshape(128, -1).astype(np.float32)
def f(rng, *shape):
    return mx_ref.flush((rng.standard_normal(shape, dtype=np.float32) * np.exp2(rng.integers(-2, 3, shape[:-1] + (1,)))).astype(BF))
def wide(rng, *shape, cols=0):
    v = rng.standard_normal(shape, dtype=np.float32) * np.exp2(rng.integers(-12, 13, shape)).astype(np.float32)
    if cols: v *= np.repeat(np.exp2(rng.integers(-cols, cols + 1, shape[:-2] + (1, shape[-1] // 4))) * (rng.random(shape[:-2] + (1, shape[-1] // 4)) > 0.0625), 4, axis=-1).astype(np.float32)
    return mx_ref.flush(v.astype(BF))
C, K, M, R = 384, 128, 16, 3
STEP = [1, 2, 4]
def order(s, k):
    s, k = s + np.float32(0.0), k + np.float32(0.0)
    best = np.argsort(-s[:, 1:], axis=1, kind="stable")[:, :M - 1] + 1
    head = np.sort(np.concatenate([np.zeros((8, 1), np.int64), best], axis=1), axis=1)
    last = np.concatenate([head[:, 1:] - 1, np.full((8, 1), C - 1)], axis=1)
    key = np.take_along_axis(k, head, axis=1)
    turn = key < np.take_along_axis(k, last, axis=1)
    run = np.argsort(-key, axis=1, kind="stable")
    return np.stack([np.concatenate([np.arange(head[g, n], last[g, n] + 1)[::-1 if turn[g, n] else 1] for n in run[g]]) for g in range(8)])
def strip(v):
    v = v.astype(np.float32)
    v[np.abs(v) < np.float32(2.0 ** -16)] = 0
    return v.astype(BF)
def numbers_of(rng):
    return {"x": strip(f(rng, N, 128, 4 * C)), "u": np.array(f(rng, N, 128, 512)), "v": np.array(f(rng, N, 128, 512))}
def weights(rng, e=slice(0, 0)):
    w = np.array(f(rng, N, 128, 2048)).reshape(N, 8, 16, 4, 8, 16, 4)
    w[:, :, e] = 0
    w[:, :, :, :, :, e] = 0
    c, p = packed(w.reshape(N, 128, 2048), rng)
    return {"wc": c, "ws": p}
def signs(rng):
    return np.stack([rng.permutation(8) % 2 * 2.0 - 1.0 for r in range(N)])
def small(rng):
    return np.where(rng.permutation(N) < N // 2, 2.0 ** -30, 1.0).astype(np.float32)
def setup_inputs(rng):
    return {**numbers_of(rng), **weights(rng)}
def setup_inputs_ties(rng):
    d = numbers_of(rng)
    e = rng.permutation(N)
    x = d["x"].reshape(N, 8, 16, C, 4)
    for r in range(N):
        k = np.zeros(C, int) if r == e[0] else rng.permutation(C) % 3
        a = x[r][:, :8, :3].copy()
        a[:, :, 2] = 0
        x[r][:, :8] = a[:, :, k]
    x[e[1]] = 0
    u = d["u"].reshape(N, 128, 128, 4)
    for g in range(0, 128, 16):
        for h in (g, g + 1):
            a = u[:, g:g + 8, h].copy()
            u[:, :, h] = 0
            u[:, g:g + 8, h] = a
    return {"x": x.reshape(N, 128, 4 * C), "u": u.reshape(N, 128, 512), "v": d["v"], **weights(rng, slice(0, 8))}
def setup_inputs_near(rng):
    d = numbers_of(rng)
    x = d["x"].astype(np.float32).reshape(N, 8, 16, C, 4)
    s = np.zeros((N, 8, C), np.int64)
    s[:, :, 1:] = (1 + np.argsort(rng.random((N, 8, C - 1)), axis=2)) // 2
    k = rng.integers(0, 12, (N, 8, C))
    digit = np.exp2(np.arange(8) - 23.0)
    a = ((s[..., None] >> np.arange(8)) & 1) * digit
    x[:, :, 0] = 0
    x[:, :, 0, :, 0] = signs(rng)[:, :, None]
    x[:, :, 8] = a[..., :4]
    x[:, :, 9] = a[..., 4:]
    x[:, :, 10] = ((k[..., None] >> np.arange(4)) & 1) * digit[:4]
    x[:, :, 11:] = rng.integers(4, 8, (N, 8, 5, C, 4)) * rng.choice([-1.0, 1.0], (N, 8, 5, C, 4)) * 2.0 ** -20
    u = d["u"].reshape(N, 128, 128, 4)
    one = small(rng).astype(BF)
    u[:, :, ::16] = 0
    u[:, :, 1::16] = 0
    for h in range(0, 128, 16):
        u[:, h, h, 0] = one
        u[:, h, h + 1, 0] = one
        u[:, h + 8:h + 10, h] = one[:, None, None]
        u[:, h + 10, h + 1] = one[:, None]
    return {"x": x.reshape(N, 128, 4 * C).astype(BF), "u": u.reshape(N, 128, 512), "v": d["v"], **weights(rng, np.r_[0, 8:16])}
def setup_inputs_runs(rng):
    d = numbers_of(rng)
    x = d["x"].astype(np.float32).reshape(N, 8, 16, C, 4)
    x[:, :, :8] = rng.integers(1, 4, (N, 8, 8, C, 4))
    x[:, :, :2] = 0
    for r in range(N):
        kind = rng.permutation(8)
        for g in range(8):
            i = kind[g] % 4
            lo, hi = ((1, M), (C - M + 1, C), (K + 1, C), (1, C))[i]
            e = lo + rng.permutation(hi - lo)[:M - 1]
            s = rng.integers(-1, 2, C) * 1.0
            s[e] = 1.25
            s[0] = 3
            k = rng.integers(-4, 4, C)
            if i == 0: k = 3 - np.arange(C) * 8 // C
            if i == 1: k = np.arange(C) * 8 // C - 4
            if i == 2:
                k = rng.integers(-4, 2, C) * 1.0
                k[0] = 2
                if kind[g] > 3: k[np.min(e) - 1] = 2.5
            x[r, g, 0, :, 0] = s
            x[r, g, 1, :, 0] = k
    one = small(rng)
    x[:, :, :8] *= one[:, None, None, None, None]
    u = d["u"].reshape(N, 128, 128, 4)
    u[:, :, ::16] = 0
    u[:, :, 1::16] = 0
    for h in range(0, 128, 16):
        u[:, h, h, 0] = one.astype(BF)
        u[:, h + 1, h + 1, 0] = one.astype(BF)
    return {"x": x.reshape(N, 128, 4 * C).astype(BF), "u": u.reshape(N, 128, 512), "v": d["v"], **weights(rng, slice(0, 8))}
def setup_inputs_huge(rng):
    d = numbers_of(rng)
    o = rng.permutation(N)
    x = 0.8 + 0.2 * rng.random((N, 128, C, 4))
    most = np.where(rng.random((128, C, 4)) < 0.03125, 0.9375, 1.0)
    most[:, rng.permutation(C) % 4 == 0] = 1
    x[o == 0] = most
    c = np.stack([rng.permutation(C) % 2 * 2.0 - 1.0 for r in range(N)])
    c[o < N // 2] = 1
    x *= 2.0 ** 30 * c[:, None, :, None]
    u = d["u"].reshape(N, 128, 128, 4)
    for i in range(2):
        a = 1 - 0.125 * rng.random((N, 128, 8, 4))
        a[o == 0] = 1
        a *= 2.0 ** 30 * signs(rng)[:, None, :, None]
        u[:, :, i::16] = a.astype(np.float32).astype(BF)
    return {"x": x.astype(np.float32).reshape(N, 128, 4 * C).astype(BF), "u": u.reshape(N, 128, 512), "v": d["v"], **weights(rng, slice(0, 16))}
def setup_inputs_spread(rng):
    d = setup_inputs(rng)
    d["x"] = strip(wide(rng, N, 128, 4 * C, cols=6))
    return d
def check_inputs(d):
    b = []
    for k in ("x", "u", "v"):
        a = np.abs(d[k].astype(np.float32))
        if not (np.isfinite(a).all() and ((a == 0) | (a >= 2.0 ** -30) & (a <= 2.0 ** 30)).all()): b.append("a value of " + k)
    return b
def reference(x, u, v, wc, ws):
    qu = [mx_ref.quantize(u[r]) for r in range(N)]
    lay = [pk(wc[r], ws[r]) for r in range(N)]
    now = [x[r] for r in range(N)]
    for t in range(R):
        o, border = [], []
        for r in range(N):
            p = mx_ref.matmul(qu[r], mx_ref.quantize(now[r]))
            o.append(order(p[::16], p[1::16]))
            border.append(mx_ref.quantize(gcols(now[r], o[r][:, :K])))
        came = decode(join(*border)).astype(BF)
        for r in range(N):
            e = np.concatenate([cut(came, r ^ STEP[t], 4 * K), gcols(now[r], o[r][:, K:])], axis=1)
            q = mx_ref.quantize(np.ascontiguousarray(e))
            h = [np.maximum(mx_ref.matmul(pick(lay[r], np.arange(128 * b, 128 * b + 128)), q), np.float32(0.0)) * np.float32(0.015625) for b in range(4)]
            now[r] = (e.astype(np.float32) + np.stack(h, axis=2).reshape(128, -1)).astype(BF)
    y, ol = np.zeros((N, 128, C), np.float32), np.zeros((N, 8, C), np.float32)
    oc, osc = np.zeros((N, 128, 4 * C), np.uint8), np.zeros((N, 16, C), np.uint8)
    for r in range(N):
        q = mx_ref.quantize(now[r])
        y[r] = mx_ref.matmul(mx_ref.quantize(v[r]), q)
        ol[r] = o[r]
        oc[r], osc[r] = emit(q)
    return {"y": y, "ol": ol, "oc": oc, "osc": osc}

@@ -1,0 +1,547 @@
+from concourse.mybir import dt, AluOpType, AxisListType, ActivationFunctionType
+
+C, K, R = 384, 128, 3
+STEP = [1, 2, 4]
+BIG = 1.0e29
+LOW = -8000000
+SPAN = 8192
+ROUND = 1.5 * 2.0 ** 23 * SPAN
+SW = 193
+CUT = 232
+ZW = 776
+X4, F32, BF, U8, U16, I32 = "float8_e4m3fn_x4", "float32", "bfloat16", "uint8", "uint16", "int32"
+
+SCRATCH = {"ps": ("psum", [128, 4096], F32)}
+
+
+def _sb(name, n, dtype):
+    SCRATCH[name] = ("sbuf", [128, n], dtype)
+
+
+for _t in range(R + 1):
+    _sb("x%d" % _t, 4 * C, BF)
+    _sb("qx%d" % _t, C, X4)
+    _sb("sx%d" % _t, C, U8)
+for _t in range(R):
+    _sb("e%d" % _t, 4 * C, BF)
+    _sb("un%d" % _t, 4 * C, BF)
+    _sb("got%d" % _t, 32, U16)
+    for _n in "el":
+        _sb("q%s%d" % (_n, _t), C, X4)
+        _sb("s%s%d" % (_n, _t), C, U8)
+    _sb("qh%d" % _t, K, X4)
+    _sb("sh%d" % _t, K, U8)
+    _sb("lst%d" % _t, 96, U16)
+    _sb("o1_%d" % _t, 6, U16)
+    _sb("o2_%d" % _t, 2, U16)
+for _n, _w in (("u", 128), ("v", 128), ("up", 256), ("w", 512), ("id", 512)):
+    _sb("q" + _n, _w, X4)
+    _sb("s" + _n, _w, U8)
+for _n, _w, _d in (
+        ("ub", 512, BF), ("vb", 512, BF), ("idb", 2048, BF), ("dif", 128, F32), ("dif2", 128, F32),
+        ("pi", 8, I32), ("pf", 8, F32), ("uli", 16, I32), ("ul", 16, U16), ("oc16", 4, U16),
+        ("cs", 32, F32), ("row", 16, F32), ("mask", 32, F32), ("raw", 1024, F32),
+        ("kw", ZW, F32), ("t2", ZW, F32), ("cc", 96, F32), ("z", (R + 1) * ZW, F32),
+        ("ss", C, F32), ("hl", C, F32), ("mm", 23 * SW, F32), ("top", 64, F32), ("col", 8, F32),
+        ("fa", C, BF), ("fs", C, BF), ("fb", C, BF), ("cap", C, BF), ("cnt", C, BF),
+        ("gr", 96, F32), ("tt", 32, F32), ("cmp", 32, F32), ("wt", 32, F32), ("pr", 32, F32), ("ln", 16, F32),
+        ("sm", 64, F32), ("pay", 32, F32), ("pz", 32, F32), ("val", 32, F32), ("wr", C, F32),
+        ("d1", 96, F32), ("d2", 96, F32), ("d3", 96, F32), ("d4", 96, F32), ("d5", 96, F32),
+        ("rl", 4 * C, F32), ("yb", C, F32), ("r1", C, F32), ("olb", C, F32)):
+    _sb(_n, _w, _d)
+
+POOLS = {"v": 40, "s": 34, "t": 16, "g": 16, "d": 24}
+SEMAPHORES = (["%s%d" % (q, i) for q in POOLS for i in range(POOLS[q])] + ["arr%d" % k for k in range(4 * R)]
+              + ["hop%d" % t for t in range(R)] + ["sent"])
+
+A = AluOpType
+ACT = ActivationFunctionType
+SEG = [(128, 256), (256, 384), (0, 128)]
+
+
+def _meet(a, b):
+    if a[0] != b[0] or a[2] <= b[1] or b[2] <= a[1]:
+        return False
+    return not (a[3] == b[3] and a[3] > 1 and a[1] % a[3] != b[1] % b[3])
+
+
+def _clash(x, y):
+    for a in x["w"]:
+        for b in y["r"] + y["w"]:
+            if _meet(a, b):
+                return True
+    for a in x["r"]:
+        for b in y["w"]:
+            if _meet(a, b):
+                return True
+    return x["q"] != y["q"] and bool(x["banks"] & y["banks"])
+
+
+def _emit(ops, g, T):
+    queue = {"v": g.vector, "s": g.scalar, "t": g.tensor, "g": g, "y": g.sync}
+    known = {q: 0 for q in queue}
+    for i, o in enumerate(ops):
+        o["waits"] = []
+        k = known[o["q"]]
+        for j in range(i - 1, -1, -1):
+            if not k >> j & 1 and (j in o["after"] or _clash(ops[j], o)):
+                o["waits"].append(j)
+                ops[j]["inc"] = True
+                k |= ops[j]["done"]
+        known[o["q"]] = k
+        o["seen"] = k
+        o["done"] = k | 1 << i
+    last = {p: [] for p in POOLS}
+    for i, o in enumerate(ops):
+        e = queue[o["q"]]
+        for j in reversed(o["waits"]):
+            e.wait_ge(T.sem[ops[j]["sem"]], ops[j]["count"])
+        for s, n in o["ext"]:
+            e.wait_ge(T.sem[s], n)
+        if o["fn"] is None:
+            continue
+        ins = o["fn"](e)
+        if o["inc"]:
+            pool = "d" if o["dma"] else o["q"]
+            step = 16 if o["dma"] else 1
+            use = last[pool]
+            free = [s for s in range(len(use)) if o["seen"] >> use[s][0] & 1]
+            if free:
+                s = free[0]
+                use[s] = (i, use[s][1] + step)
+            else:
+                s = len(use)
+                assert s < POOLS[pool], pool
+                use.append((i, step))
+            o["sem"], o["count"] = "%s%d" % (pool, s), use[s][1]
+            ins.then_inc(T.sem[o["sem"]], step)
+
+
+def _mate(T, core, t):
+    return T.cores[T.rank_of(core) ^ STEP[t]]
+
+
+def _helper(T, topo, core, t):
+    mate = _mate(T, core, t)
+    if topo.chip(mate) == topo.chip(core):
+        return None
+    here = [c for c in topo.cores_of(core) if topo.die(c) == topo.die(core)]
+    there = [c for c in topo.cores_of(core) if topo.die(c) != topo.die(core)]
+    h = there[here.index(core)]
+    return h if T.rank_of(h) is None and topo.may_write(h, mate) else None
+
+
+def _hand_on(g, core, T, topo):
+    sent = 0
+    for t in range(R):
+        for c in T.cores:
+            if _helper(T, topo, c, t) == core:
+                mate = _mate(T, c, t)
+                rid, pid = topo.addr(mate)[:2]
+                lo, hi = SEG[0]
+                g.wait_ge(T.sem["hop%d" % t], 2 * len(topo.engines(c, core)))
+                arr, mask = T.sem["arr%d" % (4 * t)], topo.mask(core, mate)
+                g.remote_dma(T["ql%d" % t][:, lo:hi].bitcast(dt.uint8), T["qh%d" % t][:].bitcast(dt.uint8),
+                             arr, T.sem.sent, pid, rid, mask)
+                g.remote_dma(T["sl%d" % t][:, lo:hi], T["sh%d" % t][:], arr, T.sem.sent, pid, rid, mask)
+                sent += 2 * len(topo.engines(core, mate))
+    if sent:
+        g.wait_ge(T.sem.sent, sent)
+
+
+def rank_program(g, core, T, topo):
+    rank = T.rank_of(core)
+    if rank is None:
+        _hand_on(g, core, T, topo)
+        return
+    ops = []
+
+    def V(name, lo=0, hi=None, step=1):
+        hi = SCRATCH[name][1][1] if hi is None else hi
+        view = T[name][:, lo:hi] if step == 1 else T[name][:, lo:hi:step]
+        return (view, [(name, lo, hi, step)])
+
+    def IND(win, off, words=False):
+        view = win[0].bitcast(dt.uint32) if words else win[0]
+        return (view.indirect(off[0]), win[1] + off[1])
+
+    def P(bank, n, at=0):
+        return V("ps", 512 * bank + at, 512 * bank + n)
+
+    def op(q, fn, w=(), r=(), dma=False, after=(), ext=()):
+        wa = [a for x in w for a in x[1]]
+        ra = [a for x in r if isinstance(x, tuple) for a in x[1]]
+        banks = set(a[1] // 512 for a in wa + ra if a[0] == "ps")
+        ops.append({"q": q, "fn": fn, "w": wa, "r": ra, "banks": banks, "dma": dma, "after": set(after),
+                    "ext": list(ext), "inc": False})
+        return len(ops) - 1
+
+    def ap(x):
+        return x[0] if isinstance(x, tuple) else x
+
+    def copy(o, i):
+        return op("v", lambda e: e.tensor_copy(o[0], i[0]), [o], [i])
+
+    def scatter(win, off, i):
+        o = IND(win, off)
+        return op("v", lambda e: e.tensor_copy(o[0], i[0]), [win], [i, off])
+
+    def tt(o, a, b, f):
+        return op("v", lambda e: e.tensor_tensor(o[0], a[0], b[0], f), [o], [a, b])
+
+    def ts(o, a, s1, f1, s2=None, f2=None):
+        if f2 is None:
+            return op("v", lambda e: e.tensor_scalar(o[0], a[0], ap(s1), None, f1), [o], [a, s1])
+        return op("v", lambda e: e.tensor_scalar(o[0], a[0], ap(s1), ap(s2), f1, f2), [o], [a, s1, s2])
+
+    def fold(o, i, f):
+        return op("v", lambda e: e.tensor_reduce(o[0], i[0], AxisListType.X, f), [o], [i])
+
+    def scan(o, d0, d1, init, f0, f1):
+        return op("v", lambda e: e.tensor_tensor_scan(o[0], d0[0], d1[0], ap(init), f0, f1), [o], [d0, d1, init])
+
+    def fill(o, c):
+        return op("v", lambda e: e.memset(o[0], c), [o])
+
+    def quant(n, lo, hi, src):
+        qq, sc, i = V("q" + n, lo, hi), V("s" + n, lo, hi), V(src, 4 * lo, 4 * hi)
+        return op("v", lambda e: e.quantize_mx(qq[0], sc[0], i[0]), [qq, sc], [i])
+
+    def act(o, i, f, bias=None, scale=None, acc=None, ext=()):
+        kw = {}
+        if bias is not None:
+            kw["bias"] = ap(bias)
+        if scale is not None:
+            kw["scale"] = ap(scale)
+        if acc is not None:
+            kw["accum_out"] = acc[0]
+        return op("s", lambda e: e.activation(o[0], i[0], f, **kw), [o] + ([acc] if acc else []), [i, bias, scale], ext=ext)
+
+    def mx(bank, sn, slo, mn, lo, hi, ext=()):
+        o = P(bank, hi - lo)
+        a, b = V("q" + sn, slo, slo + 128), V("s" + sn, slo, slo + 128)
+        c, d = V("q" + mn, lo, hi), V("s" + mn, lo, hi)
+        return op("t", lambda e: e.matmul_mx(o[0], a[0], b[0], c[0], d[0], True, True), [o], [a, b, c, d], ext=ext)
+
+    def iota(o, pattern, base, cm):
+        if SCRATCH[o[1][0][0]][2] != I32:
+            return op("g", lambda e: e.iota(o[0], pattern, base, cm, allow_small_or_imprecise_dtypes=True), [o])
+        return op("g", lambda e: e.iota(o[0], pattern, base, cm), [o])
+
+    def load(q, o, src, after=()):
+        return op(q, lambda e: e.dma_start(o[0], src), [o], dma=True, after=after)
+
+    stores = []
+
+    def store(q, dst, src, i):
+        stores.append(op(q, lambda e: e.dma_start(dst, src), [], [i], dma=True))
+
+    sent = [0]
+
+    def send(to, src, dst, sem, cast=False):
+        rid, pid = topo.addr(to)[:2]
+        sa, da = (src[0].bitcast(dt.uint8), dst[0].bitcast(dt.uint8)) if cast else (src[0], dst[0])
+        mask = topo.mask(core, to)
+        op("g", lambda q: q.remote_dma(da, sa, T.sem[sem], T.sem.sent, pid, rid, mask), [], [src])
+        sent[0] += len(topo.engines(core, to))
+
+    def came(t, k, writes):
+        mate = _mate(T, core, t)
+        via = _helper(T, topo, mate, t) if k == 0 else None
+        return [("arr%d" % (4 * t + k), writes * len(topo.engines(mate if via is None else via, core)))]
+
+    def share(t, i):
+        lo, hi = SEG[i]
+        via = _helper(T, topo, core, t) if i == 0 else None
+        if via is None:
+            to, qd, sd, sem = _mate(T, core, t), V("ql%d" % t, lo, hi), V("sl%d" % t, lo, hi), "arr%d" % (4 * t + i)
+        else:
+            to, qd, sd, sem = via, V("qh%d" % t), V("sh%d" % t), "hop%d" % t
+        send(to, V("qx%d" % t, lo, hi), qd, sem, True)
+        send(to, V("sx%d" % t, lo, hi), sd, sem)
+
+    def unpack(t, which):
+        for j, i in enumerate(which):
+            lo, hi = SEG[i]
+            for b in range(4):
+                mx(4 * (j % 2) + b, "id", 128 * b, "l%d" % t, lo, hi, ext=came(t, i, 2) if b == 0 else ())
+            for b in range(4):
+                act(V("un%d" % t, 4 * lo + b, 4 * hi, 4), P(4 * (j % 2) + b, K), ACT.Copy)
+
+    def piece(q, i):
+        lo, hi = SEG[i]
+        return load(q, V("x0", 4 * lo, 4 * hi), T.x[:, 4 * lo:4 * hi])
+
+    load("y", V("ub"), T.u[:])
+    lx = [piece("y", 0)]
+    iota(V("dif"), [[1, 128]], 0, -1)
+    iota(V("pi", 0, 2), [[0, 2]], 0, 1)
+    iota(V("uli"), [[1, 2], [16, 8]], 0, 0)
+    iota(V("cs", 18, 22), [[4, 4]], 0, 0)
+    iota(V("row"), [[1, 16]], 0, 0)
+    iota(V("cs", 16, 18), [[4 * 388, 2]], 0, 0)
+    iota(V("raw", 0, 385), [[4, 385]], -2, 0)
+    iota(V("raw", 400, 496), [[16, 96]], 0, 0)
+    act(V("dif2"), V("dif"), ACT.Abs)
+    lx += [piece("s", 1), piece("s", 2)]
+    wq = V("qw")
+    load("y", (wq[0].bitcast(dt.uint8), wq[1]), T.wc[:], after=lx)
+    load("y", V("sw"), T.ws[:])
+    load("y", V("vb"), T.v[:])
+    fill(V("idb"), 0.0)
+    fill(V("mm", 0, 23 * SW, SW), -BIG)
+    fill(V("ss", 0, 1), -BIG)
+    copy(V("ul"), V("uli"))
+    fill(V("mm", 15 * SW, 16 * SW), BIG)
+    ts(V("pi", 2, 4), V("pi", 0, 2), 15, A.bitwise_and)
+    for k, bits in enumerate((31, 3, 12)):
+        ts(V("pi", 4 + k, 5 + k), V("pi", 0, 1), bits, A.bitwise_and)
+    for b in range(4):
+        act(V("idb", 512 * b + b, 512 * (b + 1), 4), V("dif2"), ACT.Relu, bias=1.0, scale=-1.0)
+    fill(V("kw", 2 * C, 2 * C + 1), 0.0)
+    copy(V("pf", 2, 7), V("pi", 2, 7))
+    quant("id", 0, 512, "idb")
+    pn, pt, pa = V("pf", 2, 3), V("pf", 5, 6), V("pf", 6, 7)
+    theta, bound = V("cs", 10, 11), V("cs", 11, 12)
+
+    quant("u", 0, 128, "ub")
+    qo = V("qup")
+    copy((qo[0].bitcast(dt.uint32), qo[1]), IND(V("qu"), V("ul"), True))
+    act(V("sup"), IND(V("su"), V("ul")), ACT.Copy)
+
+    def scores(t, i, bank):
+        lo, hi = SEG[i]
+        mx(bank, "up", 0, "x%d" % t, lo, hi)
+        mx(bank + 1, "up", 128, "x%d" % t, lo, hi)
+        act(V("ss", max(lo, 1), lo + 64), P(bank, 64, max(lo, 1) - lo), ACT.Copy)
+
+    def pairs(i, bank):
+        lo, hi = SEG[i]
+        a, b = V("ss", lo, lo + 64), P(bank, K, 64)
+        tt(V("hl", 64 * i, 64 * i + 64), a, b, A.max)
+        tt(V("hl", 192 + 64 * i, 256 + 64 * i), a, b, A.min)
+        act(V("ss", lo + 64, hi), b, ACT.Copy)
+        act(V("kw", 2 * lo, 2 * hi, 2), P(bank + 1, K), ACT.Copy)
+
+    def rung(low, k, i):
+        me = (16 + k if low else 14 - k) * SW + 64 * i
+        up = me - SW if low else me + SW
+        at = 192 * low + 64 * i
+        scan(V("mm", me + 1, me + 65), V("hl", at, at + 64), V("mm", up, up + 64),
+             -BIG if i == 0 else V("mm", me, me + 1), A.max, A.min)
+
+    made, turn = {}, [0]
+
+    def climb(n, have, apart=3):
+        for _ in range(n):
+            best = None
+            for low in (0, 1):
+                depth = 7 if low else 15
+                for i in range(have):
+                    for k in range(depth):
+                        need = [d for d in ((low, k - 1, i), (low, k, i - 1)) if min(d) >= 0]
+                        if (low, k, i) not in made and all(d in made for d in need):
+                            far = min([turn[0] - made[d] for d in need] + [apart])
+                            rate = (far, depth - k - i)
+                            if best is None or rate > best[0]:
+                                best = (rate, (low, k, i))
+            if best is None:
+                return
+            rung(*best[1])
+            made[best[1]] = turn[0]
+            turn[0] += 1
+
+    def order(t):
+        above, acc, p4, thr, rest = [V("col", k, k + 1) for k in range(5)]
+        body, n = V("ss", 1, C), C - 1
+        made.clear()
+        tt(V("top", 48, 56), V("mm", SW - 1, 8 * SW, SW), V("mm", 16 * SW - 1, 23 * SW, SW), A.min)
+        fold(thr, V("top", 48, 56), A.max)
+        act(V("top", 0, 23), V("mm", SW - 1, 23 * SW, SW), ACT.Sign, bias=thr, scale=-1.0)
+        ts(V("fa", 0, n), body, thr, A.is_gt, -1.0, A.mult)
+        act(V("top", 24, 47), V("top", 0, 23), ACT.Relu, scale=-1.0, acc=above)
+        act(V("fs", 0, n), body, ACT.Sign, bias=thr, scale=-1.0)
+        scan(V("cap", 0, n), V("fa", 0, n), V("fa", 0, n), above, A.add, A.max)
+        ts(V("fb", 0, n), V("fs", 0, n), 0.0, A.is_le, -1.0, A.mult)
+        scan(V("cnt", 0, n), V("fb", 0, n), V("cap", 0, n), 16.0, A.add, A.max)
+        act(V("fs", 0, CUT), V("cnt", 0, CUT), ACT.Sign, bias=theta, acc=acc)
+        ts(V("fb", CUT, n), V("cnt", CUT, n), bound, A.is_gt, 2.0, A.mult)
+        fold(rest, V("fb", CUT, n), A.add)
+        unpack(t, [1, 0, 2] if t < R - 1 else [1, 0])
+        o1, o2 = V("o1_%d" % t), V("o2_%d" % t)
+        ts(o1, V("cs", 0, 6), acc, A.add, rest, A.add)
+        copy(V("gr"), IND(V("kw", 0, 2 * C + 2), o1))
+        kh, kl, ta, tb = V("gr", 0, 16), V("gr", 33, 49), V("gr", 64, 80), V("gr", 65, 81)
+        op("v", lambda e: e.transpose(T.tt[:, 0:32], T.gr[:, 0:32]), [V("tt")], [V("gr", 0, 32)])
+        tt(V("ln"), tb, ta, A.subtract)
+        mine = IND(V("tt"), V("oc16", 2, 3))
+        tt(V("cmp", 0, 16), mine, kh, A.is_lt)
+        tt(V("cmp", 16, 32), mine, kh, A.is_le)
+        tt(V("wt"), IND(V("ln"), V("oc16", 0, 2)), V("mask"), A.mult)
+        tt(V("sm", 0, 16), kh, kl, A.is_lt)
+        tt(V("pr"), V("cmp"), V("wt"), A.mult)
+        tt(V("sm", 16, 32), ta, tb, A.add)
+        fold(p4, V("pr"), A.add)
+        tt(V("sm", 32, 48), V("sm", 0, 16), V("sm", 16, 32), A.mult)
+        ts(o2, V("cs", 16, 18), p4, A.add, 0.25, A.mult)
+        tt(V("pay", 0, 16), ta, V("sm", 32, 48), A.subtract)
+        tt(V("pay", 16, 32), ta, V("sm", 32, 48), A.subtract)
+        tt(V("val"), IND(V("t2"), o2), V("pay"), A.add)
+        z0 = t * ZW
+        scatter(V("z", z0, z0 + ZW), o2, V("val"))
+        if t == 0:
+            quant("v", 0, 128, "vb")
+
+        def spread(lo, hi):
+            init = float(LOW) if lo == 0 else V("wr", lo - 1, lo)
+            scan(V("wr", lo, hi), V("z", z0 + C + lo, z0 + C + hi), V("z", z0 + lo, z0 + hi), init, A.max, A.max)
+
+        steps = [
+            lambda a, b: tt(V("d1", a, b), V("wr", 4 * a + 3, 4 * b, 4), V("cc", a, b), A.add),
+            lambda a, b: ts(V("d2", a, b), V("wr", 4 * a + 3, 4 * b, 4), ROUND, A.add, -ROUND, A.add),
+            lambda a, b: tt(V("d3", a, b), V("d1", a, b), V("d2", a, b), A.subtract),
+            lambda a, b: tt(V("d4", a, b), V("d2", a, b), V("d1", a, b), A.subtract),
+            lambda a, b: tt(V("d5", a, b), V("d3", a, b), V("d4", a, b), A.max),
+            lambda a, b: copy(V("lst%d" % t, a, b), V("d5", a, b))]
+        far, own = (0, K // 4), (K // 4, C // 4)
+        if t < R - 1:
+            spread(0, C)
+            for f in steps:
+                f(*own)
+                f(*far)
+        else:
+            spread(0, K)
+            steps[0](*far)
+            steps[1](*far)
+            spread(K, C)
+            for k, ends in ((2, far), (3, far), (0, own), (4, far), (1, own), (5, far), (2, own), (3, own), (4, own), (5, own)):
+                steps[k](*ends)
+
+    def places(t):
+        z0 = R * ZW
+        tt(V("pz", 16, 32), V("gr", 64, 80), V("sm", 32, 48), A.subtract)
+        scatter(V("z", z0, z0 + ZW), V("o2_%d" % t), V("pz"))
+        scan(V("r1"), V("z", z0, z0 + C), V("z", z0 + 388, z0 + 388 + C), 0.0, A.mult, A.add)
+
+    def layer(t, bank, lo, hi):
+        for b in range(4):
+            mx(bank + b, "w", 128 * b, "e%d" % t, lo, hi)
+
+    def relu(bank, lo, hi):
+        for b in range(4):
+            act(V("rl", C * b + lo, C * b + hi), P(bank + b, hi - lo), ACT.Relu, scale=0.015625)
+
+    def add(t, i, rows):
+        (lo, hi), xn, e = SEG[i], "x%d" % (t + 1), "e%d" % t
+        for b in rows:
+            tt(V(xn, 4 * lo + b, 4 * hi, 4), V("rl", C * b + lo, C * b + hi), V(e, 4 * lo + b, 4 * hi, 4), A.add)
+
+    def pack(t, i):
+        quant("x%d" % (t + 1), SEG[i][0], SEG[i][1], "x%d" % (t + 1))
+
+    def finish(i):
+        lo, hi = SEG[i]
+        mx(4 + i, "v", 0, "x%d" % R, lo, hi)
+        cq = V("qx%d" % R, lo, hi)
+        store("y", T.oc[:, 4 * lo:4 * hi], cq[0].bitcast(dt.uint8), cq)
+
+    def result(i, q):
+        lo, hi = SEG[i]
+        act(V("yb", lo, hi), P(4 + i, K), ACT.Copy)
+        store(q, T.y[:, lo:hi], T.yb[:, lo:hi], V("yb", lo, hi))
+
+    iota(V("raw", 512, 896), [[SPAN - 4, C]], 2, 0)
+    iota(V("t2", C, ZW), [[SPAN - 4, ZW - C]], 2 - 4 * (SPAN - 4), 0)
+    iota(V("z", 0, ZW), [[0, ZW]], LOW, 0)
+    for i in range(3):
+        quant("x0", SEG[i][0], SEG[i][1], "x0")
+        scores(0, i, 2 * i)
+        share(0, i)
+        climb(8, i)
+        if i == 0:
+            copy(V("oc16", 0, 3), V("pi", 2, 5))
+            ts(V("cs", 24, 28), V("cs", 18, 22), pa, A.is_gt, float(LOW), A.mult)
+            ts(V("mask", 0, 16), V("row"), pn, A.is_gt)
+            ts(V("mask", 16, 32), V("row"), pn, A.is_lt)
+            fill(V("pz", 0, 16), 0.0)
+        pairs(i, 2 * i)
+        climb(2, i + 1)
+    iota(V("z", ZW, R * ZW), [[0, (R - 1) * ZW]], LOW, 0)
+    iota(V("z", R * ZW, (R + 1) * ZW), [[3, 2], [0, ZW // 2]], 1, 0)
+    act(V("cs", 8, 10), V("pf", 2, 4), ACT.Sign)
+    act(theta, pn, ACT.Identity, bias=-16.5)
+    act(bound, pn, ACT.Identity, bias=16.5, scale=-1.0)
+    act(V("cs", 0, 2), V("cs", 8, 10), ACT.Identity, bias=float(CUT), scale=2.0)
+    for k, (slope, base) in enumerate(((0.0, 0.0), (-764.0, 766.0), (2.0, 1.0), (-766.0, 769.0))):
+        act(V("cs", 2 + k, 3 + k), V("cs", 8, 9), ACT.Identity, bias=base + CUT, scale=slope)
+    act(V("kw", 1, 2 * C + 2, 2), V("raw", 0, 385), ACT.Identity, bias=pt)
+    act(V("cc"), V("raw", 400, 496), ACT.Identity, bias=pa)
+    for r4 in range(4):
+        act(V("t2", r4, C, 4), V("raw", 512 + r4, 896, 4), ACT.Identity, bias=V("cs", 24 + r4, 25 + r4))
+    climb(66, 3)
+
+    for t in range(R):
+        last = t == R - 1
+        xo, e, lst = "x%d" % t, "e%d" % t, "lst%d" % t
+        order(t)
+        send(_mate(T, core, t), V(lst, 0, 32), V("got%d" % t), "arr%d" % (4 * t + 3))
+        for i in range(2):
+            lo, hi = SEG[i]
+            copy(V(e, 4 * lo, 4 * lo + 256), IND(V(xo), V(lst, lo // 4, lo // 4 + 16)))
+            act(V(e, 4 * lo + 256, 4 * hi), IND(V(xo), V(lst, lo // 4 + 16, hi // 4)), ACT.Copy)
+            quant(e, lo, hi, e)
+            layer(t, 4 * i, lo, hi)
+        relu(0, 128, 256)
+        relu(4, 256, 384)
+        border = (V(e, 0, 4 * K), IND(V("un%d" % t), V("got%d" % t)), ACT.Copy)
+        if last:
+            unpack(t, [2])
+            act(*border, ext=came(t, 3, 1))
+        add(t, 0, range(4))
+        add(t, 1, range(1))
+        pack(t, 0)
+        if last:
+            finish(0)
+            add(t, 1, range(1, 4))
+            pack(t, 1)
+            finish(1)
+            quant(e, 0, K, e)
+            layer(t, 0, 0, K)
+            places(t)
+            result(0, "y")
+            result(1, "y")
+            relu(0, 0, K)
+            act(V("olb"), V("r1"), ACT.Abs, bias=0.5, scale=0.25)
+            store("y", T.ol[:], T.olb[12:128:16, :], V("olb"))
+            add(t, 2, range(4))
+            pack(t, 2)
+            finish(2)
+            for k in range(4):
+                store("ys"[k // 2], T.osc[4 * k:4 * k + 4, :], T["sx%d" % R][32 * k:32 * k + 4, :], V("sx%d" % R))
+            result(2, "s")
+            break
+        scores(t + 1, 0, 0)
+        share(t + 1, 0)
+        add(t, 1, range(1, 4))
+        pairs(0, 0)
+        pack(t, 1)
+        scores(t + 1, 1, 4)
+        share(t + 1, 1)
+        act(*border, ext=came(t, 3, 1))
+        climb(8, 1)
+        pairs(1, 4)
+        climb(12, 2)
+        quant(e, 0, K, e)
+        layer(t, 0, 0, K)
+        relu(0, 0, K)
+        climb(9, 2)
+        add(t, 2, range(4))
+        climb(1, 2)
+        pack(t, 2)
+        scores(t + 1, 2, 4)
+        share(t + 1, 2)
+        climb(9, 2)
+        pairs(2, 4)
+        climb(66, 3, 2)
+    op("g", None, after=stores, ext=[("sent", sent[0])])
+    _emit(ops, g, T)

@@ -6,8 +6,7 @@ BIG = 1.0e29
 LOW = -8000000
 SPAN = 8192
 ROUND = 1.5 * 2.0 ** 23 * SPAN
-SW = 193
-CUT = 232
+SW = 384
 ZW = 776
 X4, F32, BF, U8, U16, I32 = "float8_e4m3fn_x4", "float32", "bfloat16", "uint8", "uint16", "int32"
 
@@ -42,7 +41,7 @@ for _n, _w, _d in (
         ("pi", 8, I32), ("pf", 8, F32), ("uli", 16, I32), ("ul", 16, U16), ("oc16", 4, U16),
         ("cs", 32, F32), ("row", 16, F32), ("mask", 32, F32), ("raw", 1024, F32),
         ("kw", ZW, F32), ("t2", ZW, F32), ("cc", 96, F32), ("z", (R + 1) * ZW, F32),
-        ("ss", C, F32), ("hl", C, F32), ("mm", 23 * SW, F32), ("top", 64, F32), ("col", 8, F32),
+        ("ss", C, F32), ("hl", 2 * K, F32), ("mm", 16 * SW, F32), ("top", 16, F32), ("col", 8, F32),
         ("fa", C, BF), ("fs", C, BF), ("fb", C, BF), ("cap", C, BF), ("cnt", C, BF),
         ("gr", 96, F32), ("tt", 32, F32), ("cmp", 32, F32), ("wt", 32, F32), ("pr", 32, F32), ("ln", 16, F32),
         ("sm", 64, F32), ("pay", 32, F32), ("pz", 32, F32), ("val", 32, F32), ("wr", C, F32),
@@ -289,10 +288,9 @@ def rank_program(g, core, T, topo):
     load("y", V("sw"), T.ws[:])
     load("y", V("vb"), T.v[:])
     fill(V("idb"), 0.0)
-    fill(V("mm", 0, 23 * SW, SW), -BIG)
-    fill(V("ss", 0, 1), -BIG)
+    fill(V("mm", SW, 16 * SW, K), -BIG)
     copy(V("ul"), V("uli"))
-    fill(V("mm", 15 * SW, 16 * SW), BIG)
+    fill(V("mm", 0, SW), BIG)
     ts(V("pi", 2, 4), V("pi", 0, 2), 15, A.bitwise_and)
     for k, bits in enumerate((31, 3, 12)):
         ts(V("pi", 4 + k, 5 + k), V("pi", 0, 1), bits, A.bitwise_and)
@@ -302,49 +300,47 @@ def rank_program(g, core, T, topo):
     copy(V("pf", 2, 7), V("pi", 2, 7))
     quant("id", 0, 512, "idb")
     pn, pt, pa = V("pf", 2, 3), V("pf", 5, 6), V("pf", 6, 7)
-    theta, bound = V("cs", 10, 11), V("cs", 11, 12)
+    theta = V("cs", 10, 11)
 
     quant("u", 0, 128, "ub")
     qo = V("qup")
     copy((qo[0].bitcast(dt.uint32), qo[1]), IND(V("qu"), V("ul"), True))
     act(V("sup"), IND(V("su"), V("ul")), ACT.Copy)
 
-    def scores(t, i, bank):
-        lo, hi = SEG[i]
-        mx(bank, "up", 0, "x%d" % t, lo, hi)
-        mx(bank + 1, "up", 128, "x%d" % t, lo, hi)
-        act(V("ss", max(lo, 1), lo + 64), P(bank, 64, max(lo, 1) - lo), ACT.Copy)
+    def score(t, i, bank, key=0):
+        mx(bank, "up", 128 * key, "x%d" % t, SEG[i][0], SEG[i][1])
 
-    def pairs(i, bank):
+    def keep(i, bank):
         lo, hi = SEG[i]
-        a, b = V("ss", lo, lo + 64), P(bank, K, 64)
-        tt(V("hl", 64 * i, 64 * i + 64), a, b, A.max)
-        tt(V("hl", 192 + 64 * i, 256 + 64 * i), a, b, A.min)
-        act(V("ss", lo + 64, hi), b, ACT.Copy)
-        act(V("kw", 2 * lo, 2 * hi, 2), P(bank + 1, K), ACT.Copy)
+        act(V("ss", max(lo, 1), hi), P(bank, K, max(lo, 1) - lo), ACT.Copy)
 
-    def rung(low, k, i):
-        me = (16 + k if low else 14 - k) * SW + 64 * i
-        up = me - SW if low else me + SW
-        at = 192 * low + 64 * i
-        scan(V("mm", me + 1, me + 65), V("hl", at, at + 64), V("mm", up, up + 64),
-             -BIG if i == 0 else V("mm", me, me + 1), A.max, A.min)
+    def keys(i, bank):
+        act(V("kw", 2 * SEG[i][0], 2 * SEG[i][1], 2), P(bank, K), ACT.Copy)
+
+    def pairs(bank):
+        tt(V("hl", 0, K), V("ss", K, 2 * K), P(bank, K), A.min)
+        tt(V("hl", K, 2 * K), V("ss", K, 2 * K), P(bank, K), A.max)
+
+    depth = (7, 15, 15)
+
+    def rung(k, i):
+        me, n = (k + 1) * SW + K * i, K - i // 2
+        data = V("hl", K * i, K * i + K) if i < 2 else P(4, K, 1)
+        scan(V("mm", me + 1, me + 1 + n), data, V("mm", me - SW, me - SW + n), V("mm", me, me + 1), A.max, A.min)
 
     made, turn = {}, [0]
 
     def climb(n, have, apart=3):
         for _ in range(n):
             best = None
-            for low in (0, 1):
-                depth = 7 if low else 15
-                for i in range(have):
-                    for k in range(depth):
-                        need = [d for d in ((low, k - 1, i), (low, k, i - 1)) if min(d) >= 0]
-                        if (low, k, i) not in made and all(d in made for d in need):
-                            far = min([turn[0] - made[d] for d in need] + [apart])
-                            rate = (far, depth - k - i)
-                            if best is None or rate > best[0]:
-                                best = (rate, (low, k, i))
+            for i in range(have):
+                for k in range(depth[i]):
+                    need = [d for d in ((k - 1, i), (k, i - 1)) if min(d) >= 0 and d[0] < depth[d[1]]]
+                    if (k, i) not in made and all(d in made for d in need):
+                        far = min([turn[0] - made[d] for d in need] + [apart])
+                        rate = (far, -k - i, i)
+                        if best is None or rate > best[0]:
+                            best = (rate, (k, i))
             if best is None:
                 return
             rung(*best[1])
@@ -352,45 +348,40 @@ def rank_program(g, core, T, topo):
             turn[0] += 1
 
     def order(t):
-        above, acc, p4, thr, rest = [V("col", k, k + 1) for k in range(5)]
-        body, n = V("ss", 1, C), C - 1
+        above, acc, p4 = [V("col", k, k + 1) for k in range(3)]
+        body, n, thr = V("ss", 1, C), C - 1, V("mm", 16 * SW - 1, 16 * SW)
         made.clear()
-        tt(V("top", 48, 56), V("mm", SW - 1, 8 * SW, SW), V("mm", 16 * SW - 1, 23 * SW, SW), A.min)
-        fold(thr, V("top", 48, 56), A.max)
-        act(V("top", 0, 23), V("mm", SW - 1, 23 * SW, SW), ACT.Sign, bias=thr, scale=-1.0)
-        ts(V("fa", 0, n), body, thr, A.is_gt, -1.0, A.mult)
-        act(V("top", 24, 47), V("top", 0, 23), ACT.Relu, scale=-1.0, acc=above)
+        act(V("top", 0, 15), V("mm", 2 * SW - 1, 16 * SW, SW), ACT.Sign, bias=thr, scale=-1.0, acc=above)
+        ts(V("fa", 0, n), body, thr, A.is_gt)
         act(V("fs", 0, n), body, ACT.Sign, bias=thr, scale=-1.0)
-        scan(V("cap", 0, n), V("fa", 0, n), V("fa", 0, n), above, A.add, A.max)
-        ts(V("fb", 0, n), V("fs", 0, n), 0.0, A.is_le, -1.0, A.mult)
-        scan(V("cnt", 0, n), V("fb", 0, n), V("cap", 0, n), 16.0, A.add, A.max)
-        act(V("fs", 0, CUT), V("cnt", 0, CUT), ACT.Sign, bias=theta, acc=acc)
-        ts(V("fb", CUT, n), V("cnt", CUT, n), bound, A.is_gt, 2.0, A.mult)
-        fold(rest, V("fb", CUT, n), A.add)
+        scan(V("cap", 0, n), V("fa", 0, n), V("fa", 0, n), above, A.add, A.min)
+        ts(V("fb", 0, n), V("fs", 0, n), 0.0, A.is_le)
+        scan(V("cnt", 0, n), V("fb", 0, n), V("cap", 0, n), -15.0, A.add, A.min)
+        act(V("fs", 0, n), V("cnt", 0, n), ACT.Sign, bias=theta, scale=-1.0, acc=acc)
         unpack(t, [1, 0, 2] if t < R - 1 else [1, 0])
+        if t == 0:
+            quant("v", 0, 128, "vb")
         o1, o2 = V("o1_%d" % t), V("o2_%d" % t)
-        ts(o1, V("cs", 0, 6), acc, A.add, rest, A.add)
+        ts(o1, V("cs", 0, 6), acc, A.add)
         copy(V("gr"), IND(V("kw", 0, 2 * C + 2), o1))
         kh, kl, ta, tb = V("gr", 0, 16), V("gr", 33, 49), V("gr", 64, 80), V("gr", 65, 81)
         op("v", lambda e: e.transpose(T.tt[:, 0:32], T.gr[:, 0:32]), [V("tt")], [V("gr", 0, 32)])
         tt(V("ln"), tb, ta, A.subtract)
+        tt(V("sm", 0, 16), kh, kl, A.is_lt)
+        tt(V("sm", 16, 32), ta, tb, A.add)
         mine = IND(V("tt"), V("oc16", 2, 3))
         tt(V("cmp", 0, 16), mine, kh, A.is_lt)
         tt(V("cmp", 16, 32), mine, kh, A.is_le)
         tt(V("wt"), IND(V("ln"), V("oc16", 0, 2)), V("mask"), A.mult)
-        tt(V("sm", 0, 16), kh, kl, A.is_lt)
-        tt(V("pr"), V("cmp"), V("wt"), A.mult)
-        tt(V("sm", 16, 32), ta, tb, A.add)
-        fold(p4, V("pr"), A.add)
         tt(V("sm", 32, 48), V("sm", 0, 16), V("sm", 16, 32), A.mult)
-        ts(o2, V("cs", 16, 18), p4, A.add, 0.25, A.mult)
+        tt(V("pr"), V("cmp"), V("wt"), A.mult)
         tt(V("pay", 0, 16), ta, V("sm", 32, 48), A.subtract)
         tt(V("pay", 16, 32), ta, V("sm", 32, 48), A.subtract)
+        fold(p4, V("pr"), A.add)
+        ts(o2, V("cs", 16, 18), p4, A.add, 0.25, A.mult)
         tt(V("val"), IND(V("t2"), o2), V("pay"), A.add)
         z0 = t * ZW
         scatter(V("z", z0, z0 + ZW), o2, V("val"))
-        if t == 0:
-            quant("v", 0, 128, "vb")
 
         def spread(lo, hi):
             init = float(LOW) if lo == 0 else V("wr", lo - 1, lo)
@@ -404,18 +395,12 @@ def rank_program(g, core, T, topo):
             lambda a, b: tt(V("d5", a, b), V("d3", a, b), V("d4", a, b), A.max),
             lambda a, b: copy(V("lst%d" % t, a, b), V("d5", a, b))]
         far, own = (0, K // 4), (K // 4, C // 4)
-        if t < R - 1:
-            spread(0, C)
-            for f in steps:
-                f(*own)
-                f(*far)
-        else:
-            spread(0, K)
-            steps[0](*far)
-            steps[1](*far)
-            spread(K, C)
-            for k, ends in ((2, far), (3, far), (0, own), (4, far), (1, own), (5, far), (2, own), (3, own), (4, own), (5, own)):
-                steps[k](*ends)
+        spread(0, K)
+        steps[0](*far)
+        steps[1](*far)
+        spread(K, C)
+        for k, ends in ((2, far), (3, far), (0, own), (1, own), (4, far), (2, own), (3, own), (5, far), (4, own), (5, own)):
+            steps[k](*ends)
 
     def places(t):
         z0 = R * ZW
@@ -423,12 +408,12 @@ def rank_program(g, core, T, topo):
         scatter(V("z", z0, z0 + ZW), V("o2_%d" % t), V("pz"))
         scan(V("r1"), V("z", z0, z0 + C), V("z", z0 + 388, z0 + 388 + C), 0.0, A.mult, A.add)
 
-    def layer(t, bank, lo, hi):
-        for b in range(4):
+    def layer(t, bank, lo, hi, rows=range(4)):
+        for b in rows:
             mx(bank + b, "w", 128 * b, "e%d" % t, lo, hi)
 
-    def relu(bank, lo, hi):
-        for b in range(4):
+    def relu(bank, lo, hi, rows=range(4)):
+        for b in rows:
             act(V("rl", C * b + lo, C * b + hi), P(bank + b, hi - lo), ACT.Relu, scale=0.015625)
 
     def add(t, i, rows):
@@ -455,30 +440,34 @@ def rank_program(g, core, T, topo):
     iota(V("z", 0, ZW), [[0, ZW]], LOW, 0)
     for i in range(3):
         quant("x0", SEG[i][0], SEG[i][1], "x0")
-        scores(0, i, 2 * i)
+        score(0, i, 2 * i)
         share(0, i)
-        climb(8, i)
         if i == 0:
+            keep(0, 0)
             copy(V("oc16", 0, 3), V("pi", 2, 5))
             ts(V("cs", 24, 28), V("cs", 18, 22), pa, A.is_gt, float(LOW), A.mult)
             ts(V("mask", 0, 16), V("row"), pn, A.is_gt)
             ts(V("mask", 16, 32), V("row"), pn, A.is_lt)
             fill(V("pz", 0, 16), 0.0)
-        pairs(i, 2 * i)
-        climb(2, i + 1)
+    score(0, 2, 5)
+    pairs(2)
+    keep(1, 2)
+    keep(2, 5)
+    for i in range(3):
+        score(0, i, (1, 3, 6)[i], 1)
+        keys(i, (1, 3, 6)[i])
     iota(V("z", ZW, R * ZW), [[0, (R - 1) * ZW]], LOW, 0)
     iota(V("z", R * ZW, (R + 1) * ZW), [[3, 2], [0, ZW // 2]], 1, 0)
     act(V("cs", 8, 10), V("pf", 2, 4), ACT.Sign)
-    act(theta, pn, ACT.Identity, bias=-16.5)
-    act(bound, pn, ACT.Identity, bias=16.5, scale=-1.0)
-    act(V("cs", 0, 2), V("cs", 8, 10), ACT.Identity, bias=float(CUT), scale=2.0)
+    act(theta, pn, ACT.Identity, bias=-15.5)
+    act(V("cs", 0, 2), V("cs", 8, 10), ACT.Identity, bias=C - 1.0, scale=2.0)
     for k, (slope, base) in enumerate(((0.0, 0.0), (-764.0, 766.0), (2.0, 1.0), (-766.0, 769.0))):
-        act(V("cs", 2 + k, 3 + k), V("cs", 8, 9), ACT.Identity, bias=base + CUT, scale=slope)
+        act(V("cs", 2 + k, 3 + k), V("cs", 8, 9), ACT.Identity, bias=base + C - 1.0, scale=slope)
     act(V("kw", 1, 2 * C + 2, 2), V("raw", 0, 385), ACT.Identity, bias=pt)
     act(V("cc"), V("raw", 400, 496), ACT.Identity, bias=pa)
     for r4 in range(4):
         act(V("t2", r4, C, 4), V("raw", 512 + r4, 896, 4), ACT.Identity, bias=V("cs", 24 + r4, 25 + r4))
-    climb(66, 3)
+    climb(37, 3)
 
     for t in range(R):
         last = t == R - 1
@@ -493,24 +482,23 @@ def rank_program(g, core, T, topo):
             layer(t, 4 * i, lo, hi)
         relu(0, 128, 256)
         relu(4, 256, 384)
-        border = (V(e, 0, 4 * K), IND(V("un%d" % t), V("got%d" % t)), ACT.Copy)
         if last:
             unpack(t, [2])
-            act(*border, ext=came(t, 3, 1))
+        act(V(e, 0, 4 * K), IND(V("un%d" % t), V("got%d" % t)), ACT.Copy, ext=came(t, 3, 1))
         add(t, 0, range(4))
         add(t, 1, range(1))
         pack(t, 0)
         if last:
             finish(0)
             add(t, 1, range(1, 4))
-            pack(t, 1)
-            finish(1)
             quant(e, 0, K, e)
             layer(t, 0, 0, K)
+            pack(t, 1)
+            finish(1)
             places(t)
+            relu(0, 0, K)
             result(0, "y")
             result(1, "y")
-            relu(0, 0, K)
             act(V("olb"), V("r1"), ACT.Abs, bias=0.5, scale=0.25)
             store("y", T.ol[:], T.olb[12:128:16, :], V("olb"))
             add(t, 2, range(4))
@@ -520,28 +508,34 @@ def rank_program(g, core, T, topo):
                 store("ys"[k // 2], T.osc[4 * k:4 * k + 4, :], T["sx%d" % R][32 * k:32 * k + 4, :], V("sx%d" % R))
             result(2, "s")
             break
-        scores(t + 1, 0, 0)
+        score(t + 1, 0, 4)
+        score(t + 1, 0, 5, 1)
+        keep(0, 4)
         share(t + 1, 0)
         add(t, 1, range(1, 4))
-        pairs(0, 0)
-        pack(t, 1)
-        scores(t + 1, 1, 4)
-        share(t + 1, 1)
-        act(*border, ext=came(t, 3, 1))
-        climb(8, 1)
-        pairs(1, 4)
-        climb(12, 2)
         quant(e, 0, K, e)
-        layer(t, 0, 0, K)
+        pack(t, 1)
+        share(t + 1, 1)
+        layer(t, 0, 0, K, range(1))
+        score(t + 1, 1, 6)
+        layer(t, 0, 0, K, range(1, 4))
+        score(t + 1, 1, 7, 1)
         relu(0, 0, K)
-        climb(9, 2)
-        add(t, 2, range(4))
-        climb(1, 2)
+        pairs(6)
+        for b in range(4):
+            add(t, 2, [b])
+            climb(1, 2, 1)
         pack(t, 2)
-        scores(t + 1, 2, 4)
+        keys(0, 5)
+        keep(1, 6)
+        keys(1, 7)
+        score(t + 1, 2, 4)
+        score(t + 1, 2, 5)
+        score(t + 1, 2, 0, 1)
+        keep(2, 5)
+        keys(2, 0)
         share(t + 1, 2)
-        climb(9, 2)
-        pairs(2, 4)
-        climb(66, 3, 2)
+        climb(3, 2, 2)
+        climb(37, 3)
     op("g", None, after=stores, ext=[("sent", sent[0])])
     _emit(ops, g, T)

@@ -7,6 +7,7 @@ LOW = -8000000
 SPAN = 8192
 ROUND = 1.5 * 2.0 ** 23 * SPAN
 SW = 384
+LAG = 3
 ZW = 776
 X4, F32, BF, U8, U16, I32 = "float8_e4m3fn_x4", "float32", "bfloat16", "uint8", "uint16", "int32"
 
@@ -259,8 +260,8 @@ def rank_program(g, core, T, topo):
         send(to, V("qx%d" % t, lo, hi), qd, sem, True)
         send(to, V("sx%d" % t, lo, hi), sd, sem)
 
-    def unpack(t, which):
-        for j, i in enumerate(which):
+    def unpack(t):
+        for j, i in enumerate((1, 0, 2)):
             lo, hi = SEG[i]
             for b in range(4):
                 mx(4 * (j % 2) + b, "id", 128 * b, "l%d" % t, lo, hi, ext=came(t, i, 2) if b == 0 else ())
@@ -321,31 +322,31 @@ def rank_program(g, core, T, topo):
         tt(V("hl", 0, K), V("ss", K, 2 * K), P(bank, K), A.min)
         tt(V("hl", K, 2 * K), V("ss", K, 2 * K), P(bank, K), A.max)
 
-    depth = (7, 15, 15)
+    depth, at = (7, 15, 15, 15, 15), (0, 128, 192, 256, 319, 383)
 
     def rung(k, i):
-        me, n = (k + 1) * SW + K * i, K - i // 2
-        data = V("hl", K * i, K * i + K) if i < 2 else P(4, K, 1)
+        me, n = (k + 1) * SW + at[i], at[i + 1] - at[i]
+        data = V("hl", at[i], at[i + 1]) if i < 3 else P(4, at[i + 1] - 255, at[i] - 255)
         scan(V("mm", me + 1, me + 1 + n), data, V("mm", me - SW, me - SW + n), V("mm", me, me + 1), A.max, A.min)
 
-    made, turn = {}, [0]
+    made, now = {}, [0]
 
-    def climb(n, have, apart=3):
+    def climb(n, have, busy=0):
+        now[0] += busy
         for _ in range(n):
             best = None
             for i in range(have):
                 for k in range(depth[i]):
                     need = [d for d in ((k - 1, i), (k, i - 1)) if min(d) >= 0 and d[0] < depth[d[1]]]
                     if (k, i) not in made and all(d in made for d in need):
-                        far = min([turn[0] - made[d] for d in need] + [apart])
-                        rate = (far, -k - i, i)
-                        if best is None or rate > best[0]:
+                        rate = (max([made[d] + LAG for d in need] + [now[0]]), k + i)
+                        if best is None or rate < best[0]:
                             best = (rate, (k, i))
             if best is None:
                 return
             rung(*best[1])
-            made[best[1]] = turn[0]
-            turn[0] += 1
+            now[0] = best[0][0] + (2 if best[1][1] == 0 else 1)
+            made[best[1]] = now[0]
 
     def order(t):
         above, acc, p4 = [V("col", k, k + 1) for k in range(3)]
@@ -358,7 +359,7 @@ def rank_program(g, core, T, topo):
         ts(V("fb", 0, n), V("fs", 0, n), 0.0, A.is_le)
         scan(V("cnt", 0, n), V("fb", 0, n), V("cap", 0, n), -15.0, A.add, A.min)
         act(V("fs", 0, n), V("cnt", 0, n), ACT.Sign, bias=theta, scale=-1.0, acc=acc)
-        unpack(t, [1, 0, 2] if t < R - 1 else [1, 0])
+        unpack(t)
         if t == 0:
             quant("v", 0, 128, "vb")
         o1, o2 = V("o1_%d" % t), V("o2_%d" % t)
@@ -378,8 +379,12 @@ def rank_program(g, core, T, topo):
         tt(V("pay", 0, 16), ta, V("sm", 32, 48), A.subtract)
         tt(V("pay", 16, 32), ta, V("sm", 32, 48), A.subtract)
         fold(p4, V("pr"), A.add)
+        if t == R - 1:
+            tt(V("pz", 16, 32), ta, V("sm", 32, 48), A.subtract)
         ts(o2, V("cs", 16, 18), p4, A.add, 0.25, A.mult)
         tt(V("val"), IND(V("t2"), o2), V("pay"), A.add)
+        if t == R - 1:
+            scatter(V("z", R * ZW, (R + 1) * ZW), o2, V("pz"))
         z0 = t * ZW
         scatter(V("z", z0, z0 + ZW), o2, V("val"))
 
@@ -402,18 +407,16 @@ def rank_program(g, core, T, topo):
         for k, ends in ((2, far), (3, far), (0, own), (1, own), (4, far), (2, own), (3, own), (5, far), (4, own), (5, own)):
             steps[k](*ends)
 
-    def places(t):
+    def places():
         z0 = R * ZW
-        tt(V("pz", 16, 32), V("gr", 64, 80), V("sm", 32, 48), A.subtract)
-        scatter(V("z", z0, z0 + ZW), V("o2_%d" % t), V("pz"))
         scan(V("r1"), V("z", z0, z0 + C), V("z", z0 + 388, z0 + 388 + C), 0.0, A.mult, A.add)
 
     def layer(t, bank, lo, hi, rows=range(4)):
         for b in rows:
             mx(bank + b, "w", 128 * b, "e%d" % t, lo, hi)
 
-    def relu(bank, lo, hi, rows=range(4)):
-        for b in rows:
+    def relu(bank, lo, hi):
+        for b in range(4):
             act(V("rl", C * b + lo, C * b + hi), P(bank + b, hi - lo), ACT.Relu, scale=0.015625)
 
     def add(t, i, rows):
@@ -467,7 +470,7 @@ def rank_program(g, core, T, topo):
     act(V("cc"), V("raw", 400, 496), ACT.Identity, bias=pa)
     for r4 in range(4):
         act(V("t2", r4, C, 4), V("raw", 512 + r4, 896, 4), ACT.Identity, bias=V("cs", 24 + r4, 25 + r4))
-    climb(37, 3)
+    climb(67, 5)
 
     for t in range(R):
         last = t == R - 1
@@ -482,8 +485,6 @@ def rank_program(g, core, T, topo):
             layer(t, 4 * i, lo, hi)
         relu(0, 128, 256)
         relu(4, 256, 384)
-        if last:
-            unpack(t, [2])
         act(V(e, 0, 4 * K), IND(V("un%d" % t), V("got%d" % t)), ACT.Copy, ext=came(t, 3, 1))
         add(t, 0, range(4))
         add(t, 1, range(1))
@@ -495,7 +496,7 @@ def rank_program(g, core, T, topo):
             layer(t, 0, 0, K)
             pack(t, 1)
             finish(1)
-            places(t)
+            places()
             relu(0, 0, K)
             result(0, "y")
             result(1, "y")
@@ -524,7 +525,7 @@ def rank_program(g, core, T, topo):
         pairs(6)
         for b in range(4):
             add(t, 2, [b])
-            climb(1, 2, 1)
+            climb(1, 3, 4)
         pack(t, 2)
         keys(0, 5)
         keep(1, 6)
@@ -535,7 +536,7 @@ def rank_program(g, core, T, topo):
         keep(2, 5)
         keys(2, 0)
         share(t + 1, 2)
-        climb(3, 2, 2)
-        climb(37, 3)
+        climb(6, 3, 2)
+        climb(67, 5)
     op("g", None, after=stores, ext=[("sent", sent[0])])
     _emit(ops, g, T)

@@ -3,13 +3,10 @@ from concourse.mybir import dt, AluOpType, AxisListType, ActivationFunctionType
 C, K, R = 384, 128, 3
 STEP = [1, 2, 4]
 BIG = 1.0e29
-LOW = -8000000
-SPAN = 8192
-ROUND = 1.5 * 2.0 ** 23 * SPAN
 SW = 384
-LAG = 3
-ZW = 776
+ZW = C + 16
 X4, F32, BF, U8, U16, I32 = "float8_e4m3fn_x4", "float32", "bfloat16", "uint8", "uint16", "int32"
+CYC, WAKE, LOCAL, REMOTE, RATE = 0.95, 210.0, 1300.0, 1500.0, 190.0
 
 SCRATCH = {"ps": ("psum", [128, 4096], F32)}
 
@@ -19,19 +16,20 @@ def _sb(name, n, dtype):
 
 
 for _t in range(R + 1):
-    _sb("x%d" % _t, 4 * C, BF)
+    _sb("x%d" % _t, 8 * C if _t < R else 4 * C, BF)
     _sb("qx%d" % _t, C, X4)
     _sb("sx%d" % _t, C, U8)
 for _t in range(R):
     _sb("e%d" % _t, 4 * C, BF)
-    _sb("un%d" % _t, 4 * C, BF)
-    _sb("got%d" % _t, 32, U16)
+    _sb("un%d" % _t, 8 * C, BF)
+    _sb("got%d" % _t, 8, U16)
     for _n in "el":
         _sb("q%s%d" % (_n, _t), C, X4)
         _sb("s%s%d" % (_n, _t), C, U8)
     _sb("qh%d" % _t, K, X4)
     _sb("sh%d" % _t, K, U8)
-    _sb("lst%d" % _t, 96, U16)
+    _sb("lst%d" % _t, 64, U16)
+    _sb("far%d" % _t, 16, U16)
     _sb("o1_%d" % _t, 6, U16)
     _sb("o2_%d" % _t, 2, U16)
 for _n, _w in (("u", 128), ("v", 128), ("up", 256), ("w", 512), ("id", 512)):
@@ -39,24 +37,30 @@ for _n, _w in (("u", 128), ("v", 128), ("up", 256), ("w", 512), ("id", 512)):
     _sb("s" + _n, _w, U8)
 for _n, _w, _d in (
         ("ub", 512, BF), ("vb", 512, BF), ("idb", 2048, BF), ("dif", 128, F32), ("dif2", 128, F32),
-        ("pi", 8, I32), ("pf", 8, F32), ("uli", 16, I32), ("ul", 16, U16), ("oc16", 4, U16),
-        ("cs", 32, F32), ("row", 16, F32), ("mask", 32, F32), ("raw", 1024, F32),
-        ("kw", ZW, F32), ("t2", ZW, F32), ("cc", 96, F32), ("z", (R + 1) * ZW, F32),
+        ("pi", 16, I32), ("pf", 16, F32), ("uli", 16, I32), ("ul", 16, U16), ("oc16", 4, U16), ("zl", 2, U16),
+        ("cs", 32, F32), ("row", 16, F32), ("mask", 32, F32), ("raw", ZW, F32),
+        ("kw", 2 * C + 8, F32), ("z", 2 * ZW, F32),
         ("ss", C, F32), ("hl", 2 * K, F32), ("mm", 16 * SW, F32), ("top", 16, F32), ("col", 8, F32),
-        ("fa", C, BF), ("fs", C, BF), ("fb", C, BF), ("cap", C, BF), ("cnt", C, BF),
+        ("fa", C, BF), ("fs", C, BF), ("ft", C, BF), ("fb", C, BF), ("cap", C, BF), ("cnt", C, BF),
         ("gr", 96, F32), ("tt", 32, F32), ("cmp", 32, F32), ("wt", 32, F32), ("pr", 32, F32), ("ln", 16, F32),
-        ("sm", 64, F32), ("pay", 32, F32), ("pz", 32, F32), ("val", 32, F32), ("wr", C, F32),
-        ("d1", 96, F32), ("d2", 96, F32), ("d3", 96, F32), ("d4", 96, F32), ("d5", 96, F32),
-        ("rl", 4 * C, F32), ("yb", C, F32), ("r1", C, F32), ("olb", C, F32)):
+        ("sm", 64, F32), ("pz", 32, F32), ("wr", ZW, F32), ("tz", 6 * K, F32),
+        ("rl", 4 * C, F32), ("yb", C, F32), ("olb", ZW, F32)):
     _sb(_n, _w, _d)
 
-POOLS = {"v": 40, "s": 34, "t": 16, "g": 16, "d": 24}
-SEMAPHORES = (["%s%d" % (q, i) for q in POOLS for i in range(POOLS[q])] + ["arr%d" % k for k in range(4 * R)]
+POOLS = {"v": 46, "s": 34, "t": 18, "g": 16, "d": 24}
+SEMAPHORES = (["%s%d" % (q, i) for q in POOLS for i in range(POOLS[q])] + ["arr%d" % k for k in range(2 * R)]
               + ["hop%d" % t for t in range(R)] + ["sent"])
 
 A = AluOpType
 ACT = ActivationFunctionType
 SEG = [(128, 256), (256, 384), (0, 128)]
+HALF = [(0, 192), (192, C - 1)]
+ROWS = [(0, 2 * K + 16), (2 * K + 16, ZW)]
+ONV = (2, 3, 0)
+VEC = ("r0 T00 T01 T20 T21 L0 r1 L2 G00 G01 T10 T11 Q0 L1 G10 G11 G12 "
+       "A00 Q1 A01 A02 A03 Q2 P0 A10 A11 A12 A13 A20 P1 A21 A22 A23 P2")
+SCA = "G02 G03 G13 R00 R01 R02 R03 G20 G21 G22 G23 R10 R11 R12 R13 R20 R21 R22 R23"
+PLAN = {}
 
 
 def _meet(a, b):
@@ -77,14 +81,66 @@ def _clash(x, y):
     return x["q"] != y["q"] and bool(x["banks"] & y["banks"])
 
 
+def _plan(ops):
+    n = len(ops)
+    deps = [[j for j in range(i) if j in ops[i]["after"] or _clash(ops[j], ops[i])] for i in range(n)]
+    gap = [{j: ops[j]["lat"] + WAKE for j in deps[i] + list(ops[i]["behind"])} for i in range(n)]
+    for i in range(n):
+        for j in ops[i]["follow"]:
+            gap[i].setdefault(j, ops[j]["cost"])
+    succ = [[] for _ in range(n)]
+    for i in range(n):
+        for j in gap[i]:
+            succ[j].append(i)
+    left = [len(d) for d in gap]
+    walk = [i for i in range(n) if not left[i]]
+    for i in walk:
+        for j in succ[i]:
+            left[j] -= 1
+            if not left[j]:
+                walk.append(j)
+    assert len(walk) == n
+    tail = [0.0] * n
+    for i in reversed(walk):
+        tail[i] = max([ops[i]["lat"]] + [gap[j][i] + tail[j] for j in succ[i]])
+    left = [len(d) for d in gap]
+    ready = {i: 0.0 for i in range(n) if not left[i]}
+    free = {q: 0.0 for q in "vstgy"}
+    order, start = [], [0.0] * n
+    while ready:
+        now, q = min((max(free[ops[i]["q"]], at), ops[i]["q"]) for i, at in ready.items())
+        near = sorted((-tail[i], i, max(now, at)) for i, at in ready.items() if ops[i]["q"] == q and at <= now + WAKE)
+        _, top, when = near[0]
+        at, i = when, top
+        for _, c, t in near[1:]:
+            if t < when and (max(t + tail[c], max(when, t + ops[c]["cost"]) + tail[top])
+                             <= max(when + tail[top], when + ops[top]["cost"] + tail[c])):
+                at, i = t, c
+                break
+        del ready[i]
+        order.append(i)
+        start[i] = at
+        free[q] = at + ops[i]["cost"]
+        for j in succ[i]:
+            left[j] -= 1
+            if not left[j]:
+                ready[j] = max(start[k] + gap[j][k] for k in gap[j])
+    return order, deps
+
+
 def _emit(ops, g, T):
+    if not PLAN:
+        PLAN["order"], PLAN["deps"] = _plan(ops)
+    order, deps = PLAN["order"], PLAN["deps"]
+    place = {i: k for k, i in enumerate(order)}
     queue = {"v": g.vector, "s": g.scalar, "t": g.tensor, "g": g, "y": g.sync}
     known = {q: 0 for q in queue}
-    for i, o in enumerate(ops):
+    for i in order:
+        o = ops[i]
         o["waits"] = []
         k = known[o["q"]]
-        for j in range(i - 1, -1, -1):
-            if not k >> j & 1 and (j in o["after"] or _clash(ops[j], o)):
+        for j in sorted(deps[i], key=lambda j: -place[j]):
+            if not k >> j & 1:
                 o["waits"].append(j)
                 ops[j]["inc"] = True
                 k |= ops[j]["done"]
@@ -92,7 +148,8 @@ def _emit(ops, g, T):
         o["seen"] = k
         o["done"] = k | 1 << i
     last = {p: [] for p in POOLS}
-    for i, o in enumerate(ops):
+    for i in order:
+        o = ops[i]
         e = queue[o["q"]]
         for j in reversed(o["waits"]):
             e.wait_ge(T.sem[ops[j]["sem"]], ops[j]["count"])
@@ -140,7 +197,7 @@ def _hand_on(g, core, T, topo):
                 rid, pid = topo.addr(mate)[:2]
                 lo, hi = SEG[0]
                 g.wait_ge(T.sem["hop%d" % t], 2 * len(topo.engines(c, core)))
-                arr, mask = T.sem["arr%d" % (4 * t)], topo.mask(core, mate)
+                arr, mask = T.sem["arr%d" % (2 * t)], topo.mask(core, mate)
                 g.remote_dma(T["ql%d" % t][:, lo:hi].bitcast(dt.uint8), T["qh%d" % t][:].bitcast(dt.uint8),
                              arr, T.sem.sent, pid, rid, mask)
                 g.remote_dma(T["sl%d" % t][:, lo:hi], T["sh%d" % t][:], arr, T.sem.sent, pid, rid, mask)
@@ -159,55 +216,77 @@ def rank_program(g, core, T, topo):
     def V(name, lo=0, hi=None, step=1):
         hi = SCRATCH[name][1][1] if hi is None else hi
         view = T[name][:, lo:hi] if step == 1 else T[name][:, lo:hi:step]
-        return (view, [(name, lo, hi, step)])
+        return (view, [(name, lo, hi, step)], len(range(lo, hi, step)), 0.5 if SCRATCH[name][2] in (BF, U16) else 1.0)
+
+    def BACK(name, hi, n):
+        return (T[name][:, hi:hi - n:-1], [(name, hi - n + 1, hi + 1, 1)], n, 1.0)
+
+    def X(t, lo, hi, step=1):
+        at = 4 * C if t < R else 0
+        return V("x%d" % t, at + lo, at + hi, step)
 
     def IND(win, off, words=False):
         view = win[0].bitcast(dt.uint32) if words else win[0]
-        return (view.indirect(off[0]), win[1] + off[1])
+        return (view.indirect(off[0]), win[1] + off[1], 16 * off[2], None)
 
     def P(bank, n, at=0):
         return V("ps", 512 * bank + at, 512 * bank + n)
 
-    def op(q, fn, w=(), r=(), dma=False, after=(), ext=()):
+    def op(q, fn, w=(), r=(), cost=60.0, lat=None, dma=False, after=(), behind=(), ext=()):
         wa = [a for x in w for a in x[1]]
         ra = [a for x in r if isinstance(x, tuple) for a in x[1]]
         banks = set(a[1] // 512 for a in wa + ra if a[0] == "ps")
         ops.append({"q": q, "fn": fn, "w": wa, "r": ra, "banks": banks, "dma": dma, "after": set(after),
-                    "ext": list(ext), "inc": False})
+                    "behind": set(behind), "follow": [], "ext": list(ext), "inc": False, "cost": cost,
+                    "lat": cost if lat is None else lat})
         return len(ops) - 1
+
+    def turns(calls):
+        for a, b in zip(calls, calls[1:]):
+            ops[b]["follow"].append(a)
 
     def ap(x):
         return x[0] if isinstance(x, tuple) else x
 
-    def copy(o, i):
-        return op("v", lambda e: e.tensor_copy(o[0], i[0]), [o], [i])
+    def time(i, *more, each=None):
+        if i[3] is None:
+            return 55.0 + 1.6 * CYC * i[2]
+        return CYC * max(64.0, i[2] * (each or max(x[3] for x in (i,) + more)))
+
+    def copy(o, i, **more):
+        return op("v", lambda e: e.tensor_copy(o[0], i[0]), [o], [i], time(i, o), **more)
 
     def scatter(win, off, i):
         o = IND(win, off)
-        return op("v", lambda e: e.tensor_copy(o[0], i[0]), [win], [i, off])
+        return op("v", lambda e: e.tensor_copy(o[0], i[0]), [win], [i, off], 55.0 + 3.8 * CYC * i[2])
 
     def tt(o, a, b, f):
-        return op("v", lambda e: e.tensor_tensor(o[0], a[0], b[0], f), [o], [a, b])
+        each = 1.0 if b[1][0][0] == "ps" else 2.0
+        return op("v", lambda e: e.tensor_tensor(o[0], a[0], b[0], f), [o], [a, b], time(a, each=each))
 
     def ts(o, a, s1, f1, s2=None, f2=None):
         if f2 is None:
-            return op("v", lambda e: e.tensor_scalar(o[0], a[0], ap(s1), None, f1), [o], [a, s1])
-        return op("v", lambda e: e.tensor_scalar(o[0], a[0], ap(s1), ap(s2), f1, f2), [o], [a, s1, s2])
+            return op("v", lambda e: e.tensor_scalar(o[0], a[0], ap(s1), None, f1), [o], [a, s1], time(a, o))
+        return op("v", lambda e: e.tensor_scalar(o[0], a[0], ap(s1), ap(s2), f1, f2), [o], [a, s1, s2], time(a, o))
 
     def fold(o, i, f):
-        return op("v", lambda e: e.tensor_reduce(o[0], i[0], AxisListType.X, f), [o], [i])
+        return op("v", lambda e: e.tensor_reduce(o[0], i[0], AxisListType.X, f), [o], [i], time(i, each=1.0))
 
     def scan(o, d0, d1, init, f0, f1):
-        return op("v", lambda e: e.tensor_tensor_scan(o[0], d0[0], d1[0], ap(init), f0, f1), [o], [d0, d1, init])
+        return op("v", lambda e: e.tensor_tensor_scan(o[0], d0[0], d1[0], ap(init), f0, f1), [o], [d0, d1, init],
+                  time(d0, d1, o))
+
+    def turn(o, i):
+        return op("v", lambda e: e.transpose(o[0], i[0]), [o], [i], time(i))
 
     def fill(o, c):
-        return op("v", lambda e: e.memset(o[0], c), [o])
+        return op("v", lambda e: e.memset(o[0], c), [o], [], time(o))
 
-    def quant(n, lo, hi, src):
-        qq, sc, i = V("q" + n, lo, hi), V("s" + n, lo, hi), V(src, 4 * lo, 4 * hi)
-        return op("v", lambda e: e.quantize_mx(qq[0], sc[0], i[0]), [qq, sc], [i])
+    def quant(n, lo, hi, i, **more):
+        qq, sc = V("q" + n, lo, hi), V("s" + n, lo, hi)
+        return op("v", lambda e: e.quantize_mx(qq[0], sc[0], i[0]), [qq, sc], [i], 15.0 + 0.26 * i[2], **more)
 
-    def act(o, i, f, bias=None, scale=None, acc=None, ext=()):
+    def act(o, i, f, bias=None, scale=None, acc=None, **more):
         kw = {}
         if bias is not None:
             kw["bias"] = ap(bias)
@@ -215,328 +294,269 @@ def rank_program(g, core, T, topo):
             kw["scale"] = ap(scale)
         if acc is not None:
             kw["accum_out"] = acc[0]
-        return op("s", lambda e: e.activation(o[0], i[0], f, **kw), [o] + ([acc] if acc else []), [i, bias, scale], ext=ext)
+        return op("s", lambda e: e.activation(o[0], i[0], f, **kw), [o] + ([acc] if acc else []), [i, bias, scale],
+                  time(i, each=1.0), **more)
 
-    def mx(bank, sn, slo, mn, lo, hi, ext=()):
+    def mx(bank, sn, slo, mn, lo, hi, **more):
         o = P(bank, hi - lo)
         a, b = V("q" + sn, slo, slo + 128), V("s" + sn, slo, slo + 128)
         c, d = V("q" + mn, lo, hi), V("s" + mn, lo, hi)
-        return op("t", lambda e: e.matmul_mx(o[0], a[0], b[0], c[0], d[0], True, True), [o], [a, b, c, d], ext=ext)
+        return op("t", lambda e: e.matmul_mx(o[0], a[0], b[0], c[0], d[0], True, True), [o], [a, b, c, d],
+                  0.7 * (hi - lo + 16), **more)
 
     def iota(o, pattern, base, cm):
+        cost = 130.0 + 2 * CYC * o[2]
         if SCRATCH[o[1][0][0]][2] != I32:
-            return op("g", lambda e: e.iota(o[0], pattern, base, cm, allow_small_or_imprecise_dtypes=True), [o])
-        return op("g", lambda e: e.iota(o[0], pattern, base, cm), [o])
+            return op("g", lambda e: e.iota(o[0], pattern, base, cm, allow_small_or_imprecise_dtypes=True), [o], [], cost)
+        return op("g", lambda e: e.iota(o[0], pattern, base, cm), [o], [], cost)
 
-    def load(q, o, src, after=()):
-        return op(q, lambda e: e.dma_start(o[0], src), [o], dma=True, after=after)
+    loaded = [0]
+
+    def load(q, o, src, size, after=()):
+        loaded[0] += size
+        return op(q, lambda e: e.dma_start(o[0], src), [o], [], 60.0, LOCAL + loaded[0] / RATE, dma=True, after=after)
 
     stores = []
 
-    def store(q, dst, src, i):
-        stores.append(op(q, lambda e: e.dma_start(dst, src), [], [i], dma=True))
+    def store(q, dst, src, i, size=0):
+        stores.append(op(q, lambda e: e.dma_start(dst, src), [], [i], 60.0 + size / RATE, LOCAL + size / RATE, dma=True))
 
     sent = [0]
 
     def send(to, src, dst, sem, cast=False):
         rid, pid = topo.addr(to)[:2]
         sa, da = (src[0].bitcast(dt.uint8), dst[0].bitcast(dt.uint8)) if cast else (src[0], dst[0])
-        mask = topo.mask(core, to)
-        op("g", lambda q: q.remote_dma(da, sa, T.sem[sem], T.sem.sent, pid, rid, mask), [], [src])
+        mask, first = topo.mask(core, to), not sent[0]
         sent[0] += len(topo.engines(core, to))
+        return op("g", lambda q: q.remote_dma(da, sa, T.sem[sem], T.sem.sent, pid, rid, mask), [], [src],
+                  REMOTE if first else 100.0, REMOTE * (2 if cast else 1))
 
-    def came(t, k, writes):
-        mate = _mate(T, core, t)
-        via = _helper(T, topo, mate, t) if k == 0 else None
-        return [("arr%d" % (4 * t + k), writes * len(topo.engines(mate if via is None else via, core)))]
+    shared = {t: [] for t in range(R)}
 
     def share(t, i):
         lo, hi = SEG[i]
         via = _helper(T, topo, core, t) if i == 0 else None
         if via is None:
-            to, qd, sd, sem = _mate(T, core, t), V("ql%d" % t, lo, hi), V("sl%d" % t, lo, hi), "arr%d" % (4 * t + i)
+            to, qd, sd, sem = _mate(T, core, t), V("ql%d" % t, lo, hi), V("sl%d" % t, lo, hi), "arr%d" % (2 * t)
         else:
             to, qd, sd, sem = via, V("qh%d" % t), V("sh%d" % t), "hop%d" % t
-        send(to, V("qx%d" % t, lo, hi), qd, sem, True)
-        send(to, V("sx%d" % t, lo, hi), sd, sem)
+        shared[t].append(send(to, V("qx%d" % t, lo, hi), qd, sem, True))
+        shared[t].append(send(to, V("sx%d" % t, lo, hi), sd, sem))
 
-    def unpack(t):
-        for j, i in enumerate((1, 0, 2)):
-            lo, hi = SEG[i]
-            for b in range(4):
-                mx(4 * (j % 2) + b, "id", 128 * b, "l%d" % t, lo, hi, ext=came(t, i, 2) if b == 0 else ())
-            for b in range(4):
-                act(V("un%d" % t, 4 * lo + b, 4 * hi, 4), P(4 * (j % 2) + b, K), ACT.Copy)
+    def unpack(t, ends):
+        mate = _mate(T, core, t)
+        via = _helper(T, topo, mate, t)
+        came = 4 * len(topo.engines(mate, core)) + 2 * len(topo.engines(mate if via is None else via, core))
+        first = mx(0, "id", 0, "l%d" % t, 0, C, ext=[("arr%d" % (2 * t), came)], behind=shared[t])
+        for b in range(1, 4):
+            mx(b, "id", 128 * b, "l%d" % t, 0, C, behind=[first])
+        for b in range(4):
+            at = C * (2 * b + 1)
+            for lo, hi in ((0, C // 2), (C // 2, C)):
+                act(V("un%d" % t, at + lo, at + hi), P(b, hi, lo), ACT.Copy, behind=[ends])
+                lo = max(lo, 1)
+                act(BACK("un%d" % t, at - lo, hi - lo), P(b, hi, lo), ACT.Copy, behind=[ends])
 
-    def piece(q, i):
-        lo, hi = SEG[i]
-        return load(q, V("x0", 4 * lo, 4 * hi), T.x[:, 4 * lo:4 * hi])
-
-    load("y", V("ub"), T.u[:])
-    lx = [piece("y", 0)]
-    iota(V("dif"), [[1, 128]], 0, -1)
-    iota(V("pi", 0, 2), [[0, 2]], 0, 1)
-    iota(V("uli"), [[1, 2], [16, 8]], 0, 0)
-    iota(V("cs", 18, 22), [[4, 4]], 0, 0)
-    iota(V("row"), [[1, 16]], 0, 0)
-    iota(V("cs", 16, 18), [[4 * 388, 2]], 0, 0)
-    iota(V("raw", 0, 385), [[4, 385]], -2, 0)
-    iota(V("raw", 400, 496), [[16, 96]], 0, 0)
-    act(V("dif2"), V("dif"), ACT.Abs)
-    lx += [piece("s", 1), piece("s", 2)]
+    first = [load("y", V("ub"), T.u[:], 128 * 1024)]
+    first += [load("y", X(0, 4 * lo, 4 * hi), T.x[:, 4 * lo:4 * hi], 128 * 1024) for lo, hi in SEG]
     wq = V("qw")
-    load("y", (wq[0].bitcast(dt.uint8), wq[1]), T.wc[:], after=lx)
-    load("y", V("sw"), T.ws[:])
-    load("y", V("vb"), T.v[:])
-    fill(V("idb"), 0.0)
-    fill(V("mm", SW, 16 * SW, K), -BIG)
-    copy(V("ul"), V("uli"))
-    fill(V("mm", 0, SW), BIG)
-    ts(V("pi", 2, 4), V("pi", 0, 2), 15, A.bitwise_and)
-    for k, bits in enumerate((31, 3, 12)):
-        ts(V("pi", 4 + k, 5 + k), V("pi", 0, 1), bits, A.bitwise_and)
+    turns(first + [load("y", (wq[0].bitcast(dt.uint8), wq[1]), T.wc[:], 128 * 2048, after=first),
+                   load("y", V("sw"), T.ws[:], 128 * 512), load("y", V("vb"), T.v[:], 128 * 1024)])
+    turns([iota(V("uli"), [[1, 2], [16, 8]], 0, 0), iota(V("pi", 0, 2), [[0, 2]], 0, 1),
+           iota(V("row"), [[1, 16]], 0, 0), iota(V("dif"), [[1, 128]], 0, -1), iota(V("raw"), [[4, ZW]], -2, 0)])
+    pn, pt, odd = V("pf", 2, 3), V("pf", 5, 6), V("pf", 9, 10)
+    theta = V("cs", 10, 11)
+    early = [fill(V("idb"), 0.0), copy(V("ul"), V("uli")), ts(V("pi", 2, 4), V("pi", 0, 2), 15, A.bitwise_and)]
+    early += [ts(V("pi", 4 + k, 5 + k), V("pi", 0, 1), bits, A.bitwise_and) for k, bits in enumerate((31, 3, 1, 6, 8, 16))]
+    early += [fill(V("mm", SW, 16 * SW, 64), -BIG), fill(V("mm", 0, SW), BIG), copy(V("pf", 2, 10), V("pi", 2, 10)),
+              copy(V("oc16", 0, 3), V("pi", 2, 5))]
+    turns(early)
+    fill(V("kw", 2 * C, 2 * C + 1), 0.0)
+    fill(V("pz", 0, 16), 0.0)
+    for t in range(R):
+        fill(V("x%d" % t, 0, 1), 0.0)
+        fill(V("un%d" % t, 0, 8 * C, 2 * C), 0.0)
+    ts(V("mask", 0, 16), V("row"), pn, A.is_gt)
+    ts(V("mask", 16, 32), V("row"), pn, A.is_lt)
+    ts(V("pf", 10, 11), V("pf", 6, 7), 128.0, A.mult, odd, A.add)
+    ts(V("pf", 11, 12), V("pf", 7, 8), 16.0, A.mult, V("pf", 10, 11), A.add)
+    ts(V("pf", 12, 13), V("pf", 8, 9), 0.125, A.mult, V("pf", 11, 12), A.add)
+    ts(V("zl"), V("row", 0, 3, 2), V("pf", 12, 13), A.add)
+    act(V("dif2"), V("dif"), ACT.Abs)
     for b in range(4):
         act(V("idb", 512 * b + b, 512 * (b + 1), 4), V("dif2"), ACT.Relu, bias=1.0, scale=-1.0)
-    fill(V("kw", 2 * C, 2 * C + 1), 0.0)
-    copy(V("pf", 2, 7), V("pi", 2, 7))
-    quant("id", 0, 512, "idb")
-    pn, pt, pa = V("pf", 2, 3), V("pf", 5, 6), V("pf", 6, 7)
-    theta = V("cs", 10, 11)
 
-    quant("u", 0, 128, "ub")
-    qo = V("qup")
-    copy((qo[0].bitcast(dt.uint32), qo[1]), IND(V("qu"), V("ul"), True))
-    act(V("sup"), IND(V("su"), V("ul")), ACT.Copy)
+    def late(*behind):
+        for k in range(2):
+            act(V("cs", 16 + k, 17 + k), odd, ACT.Identity, bias=4.0 * ZW * k, scale=4.0, behind=behind)
+        act(V("cs", 8, 10), V("pf", 2, 4), ACT.Sign, behind=behind)
+        act(theta, pn, ACT.Identity, bias=-15.5, behind=behind)
+        act(V("cs", 0, 2), V("cs", 8, 10), ACT.Identity, bias=C - 1.0, scale=2.0)
+        for k, (slope, base) in enumerate(((0.0, 0.0), (-764.0, 766.0), (2.0, 1.0), (-766.0, 769.0))):
+            act(V("cs", 2 + k, 3 + k), V("cs", 8, 9), ACT.Identity, bias=base + C - 1.0, scale=slope)
+        act(V("kw", 1, 2 * C + 2, 2), V("raw", 0, 385), ACT.Identity, bias=pt, behind=behind)
+
+    quant("u", 0, 128, V("ub"))
+    for k in range(2):
+        qo, off = V("qup", K * k, K * k + K), V("ul", 8 * k, 8 * k + 8)
+        copy((qo[0].bitcast(dt.uint32),) + qo[1:], IND(V("qu"), off, True))
+        act(V("sup", K * k, K * k + K), IND(V("su"), off), ACT.Copy)
 
     def score(t, i, bank, key=0):
         mx(bank, "up", 128 * key, "x%d" % t, SEG[i][0], SEG[i][1])
 
     def keep(i, bank):
         lo, hi = SEG[i]
-        act(V("ss", max(lo, 1), hi), P(bank, K, max(lo, 1) - lo), ACT.Copy)
+        return act(V("ss", max(lo, 1), hi), P(bank, K, max(lo, 1) - lo), ACT.Copy)
 
     def keys(i, bank):
-        act(V("kw", 2 * SEG[i][0], 2 * SEG[i][1], 2), P(bank, K), ACT.Copy)
+        return act(V("kw", 2 * SEG[i][0], 2 * SEG[i][1], 2), P(bank, K), ACT.Copy)
 
-    def pairs(bank):
-        tt(V("hl", 0, K), V("ss", K, 2 * K), P(bank, K), A.min)
-        tt(V("hl", K, 2 * K), V("ss", K, 2 * K), P(bank, K), A.max)
-
-    depth, at = (7, 15, 15, 15, 15), (0, 128, 192, 256, 319, 383)
+    chain = [(7, V("hl", 0, 128)), (15, V("hl", 128, 192)), (15, V("hl", 192, 256)), (15, P(4, 64, 1)), (15, P(4, 128, 64))]
 
     def rung(k, i):
-        me, n = (k + 1) * SW + at[i], at[i + 1] - at[i]
-        data = V("hl", at[i], at[i + 1]) if i < 3 else P(4, at[i + 1] - 255, at[i] - 255)
+        me, data = (k + 1) * SW + sum(c[1][2] for c in chain[:i]), chain[i][1]
+        n = data[2]
         scan(V("mm", me + 1, me + 1 + n), data, V("mm", me - SW, me - SW + n), V("mm", me, me + 1), A.max, A.min)
 
-    made, now = {}, [0]
-
-    def climb(n, have, busy=0):
-        now[0] += busy
-        for _ in range(n):
-            best = None
-            for i in range(have):
-                for k in range(depth[i]):
-                    need = [d for d in ((k - 1, i), (k, i - 1)) if min(d) >= 0 and d[0] < depth[d[1]]]
-                    if (k, i) not in made and all(d in made for d in need):
-                        rate = (max([made[d] + LAG for d in need] + [now[0]]), k + i)
-                        if best is None or rate < best[0]:
-                            best = (rate, (k, i))
-            if best is None:
-                return
-            rung(*best[1])
-            now[0] = best[0][0] + (2 if best[1][1] == 0 else 1)
-            made[best[1]] = now[0]
+    def rate(t, i):
+        share(t, i)
+        if i == 0:
+            score(t, 0, 4)
+            score(t, 0, 5, 1)
+            keep(0, 4)
+            keys(0, 5)
+        elif i == 1:
+            score(t, 1, 6)
+            score(t, 1, 7, 1)
+            tt(V("hl", 0, K), V("ss", K, 2 * K), P(6, K), A.min)
+            tt(V("hl", K, 2 * K), V("ss", K, 2 * K), P(6, K), A.max)
+            keep(1, 6)
+            keys(1, 7)
+        else:
+            score(t, 2, 4)
+            score(t, 2, 5)
+            score(t, 2, 7, 1)
+            keep(2, 5)
+            rated = keys(2, 7)
+            for d in range(15 + len(chain)):
+                for j in range(len(chain)):
+                    if 0 <= d - j < chain[j][0]:
+                        rung(d - j, j)
+            for lo, hi in SEG:
+                lo = max(4 * lo, 1)
+                act(BACK("x%d" % t, 4 * C - lo, 4 * hi - lo), X(t, lo, 4 * hi), ACT.Copy, behind=[rated])
+            for k in range(2):
+                act(V("z", ZW * k, ZW * k + ZW), V("raw"), ACT.Identity, bias=1.0 + 3 * k, scale=0.0, behind=[rated])
+            if t == 0:
+                late(rated)
 
     def order(t):
-        above, acc, p4 = [V("col", k, k + 1) for k in range(3)]
-        body, n, thr = V("ss", 1, C), C - 1, V("mm", 16 * SW - 1, 16 * SW)
-        made.clear()
-        act(V("top", 0, 15), V("mm", 2 * SW - 1, 16 * SW, SW), ACT.Sign, bias=thr, scale=-1.0, acc=above)
-        ts(V("fa", 0, n), body, thr, A.is_gt)
-        act(V("fs", 0, n), body, ACT.Sign, bias=thr, scale=-1.0)
-        scan(V("cap", 0, n), V("fa", 0, n), V("fa", 0, n), above, A.add, A.min)
-        ts(V("fb", 0, n), V("fs", 0, n), 0.0, A.is_le)
-        scan(V("cnt", 0, n), V("fb", 0, n), V("cap", 0, n), -15.0, A.add, A.min)
-        act(V("fs", 0, n), V("cnt", 0, n), ACT.Sign, bias=theta, scale=-1.0, acc=acc)
-        unpack(t)
+        above, p4 = V("col", 0, 1), V("col", 1, 2)
+        acc = [V("col", 2 + k, 3 + k) for k in range(2)]
+        thr = V("mm", 16 * SW - 1, 16 * SW)
+        n = {}
+        n["top"] = act(V("top", 0, 15), V("mm", 2 * SW - 1, 16 * SW, SW), ACT.Sign, bias=thr, scale=-1.0, acc=above)
+        for k, (lo, hi) in enumerate(HALF):
+            body, fa, fb, cap, cnt = [V("ss", lo + 1, hi + 1)] + [V(b, lo, hi) for b in ("fa", "fb", "cap", "cnt")]
+            n["fa", k] = ts(fa, body, thr, A.is_gt)
+            n["fs", k] = act(V("fs", lo, hi), body, ACT.Sign, bias=thr, scale=-1.0)
+            n["cap", k] = scan(cap, fa, fa, V("cap", lo - 1, lo) if k else above, A.add, A.min)
+            n["fb", k] = ts(fb, V("fs", lo, hi), 0.0, A.is_le)
+            n["cnt", k] = scan(cnt, fb, cap, V("cnt", lo - 1, lo) if k else -15.0, A.add, A.min)
+            act(V("ft", lo, hi), cnt, ACT.Sign, bias=theta, scale=-1.0, acc=acc[k])
+        turns([n["top"], n["fs", 0], n["fs", 1]])
+        turns([n[k] for k in (("fa", 0), ("fa", 1), ("cap", 0), ("fb", 0), ("fb", 1), ("cap", 1), ("cnt", 0), ("cnt", 1))])
         if t == 0:
-            quant("v", 0, 128, "vb")
-        o1, o2 = V("o1_%d" % t), V("o2_%d" % t)
-        ts(o1, V("cs", 0, 6), acc, A.add)
-        copy(V("gr"), IND(V("kw", 0, 2 * C + 2), o1))
+            for b in range(4):
+                quant("id", K * b, K * b + K, V("idb", 4 * K * b, 4 * K * (b + 1)), behind=[n["cnt", 0]])
+            quant("v", 0, 128, V("vb"), behind=[n["cnt", 1]])
+        o1, o2 = "o1_%d" % t, V("o2_%d" % t)
+        ts(V(o1), V("cs", 0, 6), acc[0], A.add, acc[1], A.add)
+        kw = V("kw", 0, 2 * C + 2)
+        copy(V("gr", 0, 32), IND(kw, V(o1, 0, 2)))
+        ends = act(V("gr", 64, 96), IND(kw, V(o1, 4, 6)), ACT.Copy)
+        copy(V("gr", 32, 64), IND(kw, V(o1, 2, 4)))
+        unpack(t, ends)
         kh, kl, ta, tb = V("gr", 0, 16), V("gr", 33, 49), V("gr", 64, 80), V("gr", 65, 81)
-        op("v", lambda e: e.transpose(T.tt[:, 0:32], T.gr[:, 0:32]), [V("tt")], [V("gr", 0, 32)])
-        tt(V("ln"), tb, ta, A.subtract)
-        tt(V("sm", 0, 16), kh, kl, A.is_lt)
-        tt(V("sm", 16, 32), ta, tb, A.add)
         mine = IND(V("tt"), V("oc16", 2, 3))
-        tt(V("cmp", 0, 16), mine, kh, A.is_lt)
-        tt(V("cmp", 16, 32), mine, kh, A.is_le)
-        tt(V("wt"), IND(V("ln"), V("oc16", 0, 2)), V("mask"), A.mult)
-        tt(V("sm", 32, 48), V("sm", 0, 16), V("sm", 16, 32), A.mult)
-        tt(V("pr"), V("cmp"), V("wt"), A.mult)
-        tt(V("pay", 0, 16), ta, V("sm", 32, 48), A.subtract)
-        tt(V("pay", 16, 32), ta, V("sm", 32, 48), A.subtract)
+        turns([turn(V("tt"), V("gr", 0, 32)),
+               tt(V("ln"), tb, ta, A.subtract),
+               tt(V("sm", 0, 16), kh, kl, A.is_lt),
+               tt(V("sm", 16, 32), ta, tb, A.add),
+               tt(V("cmp", 0, 16), mine, kh, A.is_lt),
+               tt(V("wt"), IND(V("ln"), V("oc16", 0, 2)), V("mask"), A.mult),
+               tt(V("cmp", 16, 32), mine, kh, A.is_le),
+               tt(V("sm", 32, 48), V("sm", 0, 16), V("sm", 16, 32), A.mult),
+               tt(V("pr"), V("cmp"), V("wt"), A.mult),
+               tt(V("pz", 16, 32), ta, V("sm", 32, 48), A.subtract)])
         fold(p4, V("pr"), A.add)
-        if t == R - 1:
-            tt(V("pz", 16, 32), ta, V("sm", 32, 48), A.subtract)
         ts(o2, V("cs", 16, 18), p4, A.add, 0.25, A.mult)
-        tt(V("val"), IND(V("t2"), o2), V("pay"), A.add)
-        if t == R - 1:
-            scatter(V("z", R * ZW, (R + 1) * ZW), o2, V("pz"))
-        z0 = t * ZW
-        scatter(V("z", z0, z0 + ZW), o2, V("val"))
+        scatter(V("z"), o2, V("pz"))
+        for k, (lo, hi) in enumerate(ROWS):
+            n["r", k] = scan(V("wr", lo, hi), V("z", lo, hi), V("z", ZW + lo, ZW + hi),
+                             V("wr", lo - 1, lo) if lo else 0.0, A.mult, A.add)
+        for i, (lo, hi) in enumerate(SEG):
+            for k in range(2):
+                n["T", i, k] = turn(V("tz", 2 * lo + K * k, 2 * lo + K * k + K), V("wr", lo + 16 * k, hi + 16 * k))
+            if i == 2:
+                n["L", i] = ts(V("far%d" % t), IND(V("tz", 0, 2 * K), V("zl", 0, 1)), 0.25, A.mult, C + 0.5, A.add)
+            else:
+                n["L", i] = ts(V("lst%d" % t, 32 * i, 32 * i + 32), IND(V("tz", 2 * lo, 2 * hi), V("zl")),
+                               4.0 * C + 2, A.add)
+        return n
 
-        def spread(lo, hi):
-            init = float(LOW) if lo == 0 else V("wr", lo - 1, lo)
-            scan(V("wr", lo, hi), V("z", z0 + C + lo, z0 + C + hi), V("z", z0 + lo, z0 + hi), init, A.max, A.max)
+    def gather(i, b, o, src, **more):
+        return copy(o, src, **more) if b < ONV[i] else act(o, src, ACT.Copy, **more)
 
-        steps = [
-            lambda a, b: tt(V("d1", a, b), V("wr", 4 * a + 3, 4 * b, 4), V("cc", a, b), A.add),
-            lambda a, b: ts(V("d2", a, b), V("wr", 4 * a + 3, 4 * b, 4), ROUND, A.add, -ROUND, A.add),
-            lambda a, b: tt(V("d3", a, b), V("d1", a, b), V("d2", a, b), A.subtract),
-            lambda a, b: tt(V("d4", a, b), V("d2", a, b), V("d1", a, b), A.subtract),
-            lambda a, b: tt(V("d5", a, b), V("d3", a, b), V("d4", a, b), A.max),
-            lambda a, b: copy(V("lst%d" % t, a, b), V("d5", a, b))]
-        far, own = (0, K // 4), (K // 4, C // 4)
-        spread(0, K)
-        steps[0](*far)
-        steps[1](*far)
-        spread(K, C)
-        for k, ends in ((2, far), (3, far), (0, own), (1, own), (4, far), (2, own), (3, own), (5, far), (4, own), (5, own)):
-            steps[k](*ends)
-
-    def places():
-        z0 = R * ZW
-        scan(V("r1"), V("z", z0, z0 + C), V("z", z0 + 388, z0 + 388 + C), 0.0, A.mult, A.add)
-
-    def layer(t, bank, lo, hi, rows=range(4)):
-        for b in rows:
-            mx(bank + b, "w", 128 * b, "e%d" % t, lo, hi)
-
-    def relu(bank, lo, hi):
+    def layer(t, i, bank, n):
+        (lo, hi), e = SEG[i], "e%d" % t
+        n["Q", i] = quant(e, lo, hi, V(e, 4 * lo, 4 * hi))
         for b in range(4):
-            act(V("rl", C * b + lo, C * b + hi), P(bank + b, hi - lo), ACT.Relu, scale=0.015625)
-
-    def add(t, i, rows):
-        (lo, hi), xn, e = SEG[i], "x%d" % (t + 1), "e%d" % t
-        for b in rows:
-            tt(V(xn, 4 * lo + b, 4 * hi, 4), V("rl", C * b + lo, C * b + hi), V(e, 4 * lo + b, 4 * hi, 4), A.add)
-
-    def pack(t, i):
-        quant("x%d" % (t + 1), SEG[i][0], SEG[i][1], "x%d" % (t + 1))
+            mx(bank + b, "w", 128 * b, e, lo, hi)
+            n["R", i, b] = act(V("rl", C * b + lo, C * b + hi), P(bank + b, K), ACT.Relu, scale=0.015625)
+            n["A", i, b] = tt(X(t + 1, 4 * lo + b, 4 * hi, 4), V("rl", C * b + lo, C * b + hi),
+                              V(e, 4 * lo + b, 4 * hi, 4), A.add)
+        n["P", i] = quant("x%d" % (t + 1), lo, hi, X(t + 1, 4 * lo, 4 * hi))
 
     def finish(i):
         lo, hi = SEG[i]
         mx(4 + i, "v", 0, "x%d" % R, lo, hi)
         cq = V("qx%d" % R, lo, hi)
-        store("y", T.oc[:, 4 * lo:4 * hi], cq[0].bitcast(dt.uint8), cq)
-
-    def result(i, q):
-        lo, hi = SEG[i]
+        store("y", T.oc[:, 4 * lo:4 * hi], cq[0].bitcast(dt.uint8), cq, 128 * 512)
         act(V("yb", lo, hi), P(4 + i, K), ACT.Copy)
-        store(q, T.y[:, lo:hi], T.yb[:, lo:hi], V("yb", lo, hi))
+        store("s" if i == 2 else "y", T.y[:, lo:hi], T.yb[:, lo:hi], V("yb", lo, hi), 128 * 512)
 
-    iota(V("raw", 512, 896), [[SPAN - 4, C]], 2, 0)
-    iota(V("t2", C, ZW), [[SPAN - 4, ZW - C]], 2 - 4 * (SPAN - 4), 0)
-    iota(V("z", 0, ZW), [[0, ZW]], LOW, 0)
-    for i in range(3):
-        quant("x0", SEG[i][0], SEG[i][1], "x0")
-        score(0, i, 2 * i)
-        share(0, i)
-        if i == 0:
-            keep(0, 0)
-            copy(V("oc16", 0, 3), V("pi", 2, 5))
-            ts(V("cs", 24, 28), V("cs", 18, 22), pa, A.is_gt, float(LOW), A.mult)
-            ts(V("mask", 0, 16), V("row"), pn, A.is_gt)
-            ts(V("mask", 16, 32), V("row"), pn, A.is_lt)
-            fill(V("pz", 0, 16), 0.0)
-    score(0, 2, 5)
-    pairs(2)
-    keep(1, 2)
-    keep(2, 5)
-    for i in range(3):
-        score(0, i, (1, 3, 6)[i], 1)
-        keys(i, (1, 3, 6)[i])
-    iota(V("z", ZW, R * ZW), [[0, (R - 1) * ZW]], LOW, 0)
-    iota(V("z", R * ZW, (R + 1) * ZW), [[3, 2], [0, ZW // 2]], 1, 0)
-    act(V("cs", 8, 10), V("pf", 2, 4), ACT.Sign)
-    act(theta, pn, ACT.Identity, bias=-15.5)
-    act(V("cs", 0, 2), V("cs", 8, 10), ACT.Identity, bias=C - 1.0, scale=2.0)
-    for k, (slope, base) in enumerate(((0.0, 0.0), (-764.0, 766.0), (2.0, 1.0), (-766.0, 769.0))):
-        act(V("cs", 2 + k, 3 + k), V("cs", 8, 9), ACT.Identity, bias=base + C - 1.0, scale=slope)
-    act(V("kw", 1, 2 * C + 2, 2), V("raw", 0, 385), ACT.Identity, bias=pt)
-    act(V("cc"), V("raw", 400, 496), ACT.Identity, bias=pa)
-    for r4 in range(4):
-        act(V("t2", r4, C, 4), V("raw", 512 + r4, 896, 4), ACT.Identity, bias=V("cs", 24 + r4, 25 + r4))
-    climb(67, 5)
-
+    for i, (lo, hi) in enumerate(SEG):
+        quant("x0", lo, hi, X(0, 4 * lo, 4 * hi))
+        rate(0, i)
     for t in range(R):
         last = t == R - 1
-        xo, e, lst = "x%d" % t, "e%d" % t, "lst%d" % t
-        order(t)
-        send(_mate(T, core, t), V(lst, 0, 32), V("got%d" % t), "arr%d" % (4 * t + 3))
-        for i in range(2):
-            lo, hi = SEG[i]
-            copy(V(e, 4 * lo, 4 * lo + 256), IND(V(xo), V(lst, lo // 4, lo // 4 + 16)))
-            act(V(e, 4 * lo + 256, 4 * hi), IND(V(xo), V(lst, lo // 4 + 16, hi // 4)), ACT.Copy)
-            quant(e, lo, hi, e)
-            layer(t, 4 * i, lo, hi)
-        relu(0, 128, 256)
-        relu(4, 256, 384)
-        act(V(e, 0, 4 * K), IND(V("un%d" % t), V("got%d" % t)), ACT.Copy, ext=came(t, 3, 1))
-        add(t, 0, range(4))
-        add(t, 1, range(1))
-        pack(t, 0)
+        xo, e, mate = "x%d" % t, "e%d" % t, _mate(T, core, t)
+        n = order(t)
+        told = send(mate, V("far%d" % t, 0, 8), V("got%d" % t), "arr%d" % (2 * t + 1))
+        for i, (lo, hi) in enumerate(SEG):
+            for b in range(4):
+                o = V(e, 4 * lo + b, 4 * hi, 4)
+                if i < 2:
+                    n["G", i, b] = gather(i, b, o, IND(V(xo), V("lst%d" % t, 32 * i + 8 * b, 32 * i + 8 * b + 8)))
+                else:
+                    n["G", i, b] = gather(i, b, o, IND(V("un%d" % t, 2 * C * b, 2 * C * (b + 1)), V("got%d" % t)),
+                                          behind=[told], ext=[("arr%d" % (2 * t + 1), len(topo.engines(mate, core)))])
+        for i in range(3):
+            layer(t, i, 4 * (i % 2), n)
+        for names in (VEC, SCA):
+            turns([n[(w[0],) + tuple(int(d) for d in w[1:])] for w in names.split()])
         if last:
-            finish(0)
-            add(t, 1, range(1, 4))
-            quant(e, 0, K, e)
-            layer(t, 0, 0, K)
-            pack(t, 1)
-            finish(1)
-            places()
-            relu(0, 0, K)
-            result(0, "y")
-            result(1, "y")
-            act(V("olb"), V("r1"), ACT.Abs, bias=0.5, scale=0.25)
-            store("y", T.ol[:], T.olb[12:128:16, :], V("olb"))
-            add(t, 2, range(4))
-            pack(t, 2)
-            finish(2)
-            for k in range(4):
-                store("ys"[k // 2], T.osc[4 * k:4 * k + 4, :], T["sx%d" % R][32 * k:32 * k + 4, :], V("sx%d" % R))
-            result(2, "s")
-            break
-        score(t + 1, 0, 4)
-        score(t + 1, 0, 5, 1)
-        keep(0, 4)
-        share(t + 1, 0)
-        add(t, 1, range(1, 4))
-        quant(e, 0, K, e)
-        pack(t, 1)
-        share(t + 1, 1)
-        layer(t, 0, 0, K, range(1))
-        score(t + 1, 1, 6)
-        layer(t, 0, 0, K, range(1, 4))
-        score(t + 1, 1, 7, 1)
-        relu(0, 0, K)
-        pairs(6)
-        for b in range(4):
-            add(t, 2, [b])
-            climb(1, 3, 4)
-        pack(t, 2)
-        keys(0, 5)
-        keep(1, 6)
-        keys(1, 7)
-        score(t + 1, 2, 4)
-        score(t + 1, 2, 5)
-        score(t + 1, 2, 0, 1)
-        keep(2, 5)
-        keys(2, 0)
-        share(t + 1, 2)
-        climb(6, 3, 2)
-        climb(67, 5)
-    op("g", None, after=stores, ext=[("sent", sent[0])])
+            act(V("olb"), V("wr"), ACT.Abs, bias=0.5, scale=0.25, behind=[n["R", 2, 3]])
+            for k in range(2):
+                store("y", T.ol[k:8:2, :], T.olb[16 * k:128:32, 16 * k:16 * k + C], V("olb"))
+        for i in range(3):
+            if last:
+                finish(i)
+            else:
+                rate(t + 1, i)
+    for k in range(4):
+        store("ys"[k // 2], T.osc[4 * k:4 * k + 4, :], T["sx%d" % R][32 * k:32 * k + 4, :], V("sx%d" % R))
+    op("g", None, after=stores, ext=[("sent", sent[0])], behind=range(len(ops)))
     _emit(ops, g, T)

from concourse.mybir import dt, AluOpType, AxisListType, ActivationFunctionType

C, K, R = 384, 128, 3
STEP = [1, 2, 4]
BIG = 1.0e29
SW = 384
ZW = C + 16
X4, F32, BF, U8, U16, I32 = "float8_e4m3fn_x4", "float32", "bfloat16", "uint8", "uint16", "int32"
CYC, WAKE, LOCAL, REMOTE, RATE = 0.95, 210.0, 1300.0, 1500.0, 190.0

SCRATCH = {"ps": ("psum", [128, 4096], F32)}


def _sb(name, n, dtype):
    SCRATCH[name] = ("sbuf", [128, n], dtype)


for _t in range(R + 1):
    _sb("x%d" % _t, 8 * C if _t < R else 4 * C, BF)
    _sb("qx%d" % _t, C, X4)
    _sb("sx%d" % _t, C, U8)
for _t in range(R):
    _sb("e%d" % _t, 4 * C, BF)
    _sb("un%d" % _t, 8 * C, BF)
    _sb("got%d" % _t, 8, U16)
    for _n in "el":
        _sb("q%s%d" % (_n, _t), C, X4)
        _sb("s%s%d" % (_n, _t), C, U8)
    _sb("qh%d" % _t, K, X4)
    _sb("sh%d" % _t, K, U8)
    _sb("lst%d" % _t, 64, U16)
    _sb("far%d" % _t, 16, U16)
    _sb("o1_%d" % _t, 6, U16)
    _sb("o2_%d" % _t, 2, U16)
for _n, _w in (("u", 128), ("v", 128), ("up", 256), ("w", 512), ("id", 512)):
    _sb("q" + _n, _w, X4)
    _sb("s" + _n, _w, U8)
for _n, _w, _d in (
        ("ub", 512, BF), ("vb", 512, BF), ("idb", 2048, BF), ("dif", 128, F32), ("dif2", 128, F32),
        ("pi", 16, I32), ("pf", 16, F32), ("uli", 16, I32), ("ul", 16, U16), ("oc16", 4, U16), ("zl", 2, U16),
        ("cs", 32, F32), ("row", 16, F32), ("mask", 32, F32), ("raw", ZW, F32),
        ("kw", 2 * C + 8, F32), ("z", 2 * ZW, F32),
        ("ss", C, F32), ("hl", 2 * K, F32), ("mm", 16 * SW, F32), ("top", 16, F32), ("col", 8, F32),
        ("fa", C, BF), ("fs", C, BF), ("ft", C, BF), ("fb", C, BF), ("cap", C, BF), ("cnt", C, BF),
        ("gr", 96, F32), ("tt", 32, F32), ("cmp", 32, F32), ("wt", 32, F32), ("pr", 32, F32), ("ln", 16, F32),
        ("sm", 64, F32), ("pz", 32, F32), ("wr", ZW, F32), ("tz", 6 * K, F32),
        ("rl", 4 * C, F32), ("yb", C, F32), ("olb", ZW, F32)):
    _sb(_n, _w, _d)

POOLS = {"v": 46, "s": 34, "t": 18, "g": 16, "d": 24}
SEMAPHORES = (["%s%d" % (q, i) for q in POOLS for i in range(POOLS[q])] + ["arr%d" % k for k in range(2 * R)]
              + ["hop%d" % t for t in range(R)] + ["sent"])

A = AluOpType
ACT = ActivationFunctionType
SEG = [(128, 256), (256, 384), (0, 128)]
HALF = [(0, 192), (192, C - 1)]
ROWS = [(0, 2 * K + 16), (2 * K + 16, ZW)]
ONV = (2, 3, 0)
VEC = ("r0 T00 T01 T20 T21 L0 r1 L2 G00 G01 T10 T11 Q0 L1 G10 G11 G12 "
       "A00 Q1 A01 A02 A03 Q2 P0 A10 A11 A12 A13 A20 P1 A21 A22 A23 P2")
SCA = "G02 G03 G13 R00 R01 R02 R03 G20 G21 G22 G23 R10 R11 R12 R13 R20 R21 R22 R23"
PLAN = {}


def _meet(a, b):
    if a[0] != b[0] or a[2] <= b[1] or b[2] <= a[1]:
        return False
    return not (a[3] == b[3] and a[3] > 1 and a[1] % a[3] != b[1] % b[3])


def _clash(x, y):
    for a in x["w"]:
        for b in y["r"] + y["w"]:
            if _meet(a, b):
                return True
    for a in x["r"]:
        for b in y["w"]:
            if _meet(a, b):
                return True
    return x["q"] != y["q"] and bool(x["banks"] & y["banks"])


def _plan(ops):
    n = len(ops)
    deps = [[j for j in range(i) if j in ops[i]["after"] or _clash(ops[j], ops[i])] for i in range(n)]
    gap = [{j: ops[j]["lat"] + WAKE for j in deps[i] + list(ops[i]["behind"])} for i in range(n)]
    for i in range(n):
        for j in ops[i]["follow"]:
            gap[i].setdefault(j, ops[j]["cost"])
    succ = [[] for _ in range(n)]
    for i in range(n):
        for j in gap[i]:
            succ[j].append(i)
    left = [len(d) for d in gap]
    walk = [i for i in range(n) if not left[i]]
    for i in walk:
        for j in succ[i]:
            left[j] -= 1
            if not left[j]:
                walk.append(j)
    assert len(walk) == n
    tail = [0.0] * n
    for i in reversed(walk):
        tail[i] = max([ops[i]["lat"]] + [gap[j][i] + tail[j] for j in succ[i]])
    left = [len(d) for d in gap]
    ready = {i: 0.0 for i in range(n) if not left[i]}
    free = {q: 0.0 for q in "vstgy"}
    order, start = [], [0.0] * n
    while ready:
        now, q = min((max(free[ops[i]["q"]], at), ops[i]["q"]) for i, at in ready.items())
        near = sorted((-tail[i], i, max(now, at)) for i, at in ready.items() if ops[i]["q"] == q and at <= now + WAKE)
        _, top, when = near[0]
        at, i = when, top
        for _, c, t in near[1:]:
            if t < when and (max(t + tail[c], max(when, t + ops[c]["cost"]) + tail[top])
                             <= max(when + tail[top], when + ops[top]["cost"] + tail[c])):
                at, i = t, c
                break
        del ready[i]
        order.append(i)
        start[i] = at
        free[q] = at + ops[i]["cost"]
        for j in succ[i]:
            left[j] -= 1
            if not left[j]:
                ready[j] = max(start[k] + gap[j][k] for k in gap[j])
    return order, deps


def _emit(ops, g, T):
    if not PLAN:
        PLAN["order"], PLAN["deps"] = _plan(ops)
    order, deps = PLAN["order"], PLAN["deps"]
    place = {i: k for k, i in enumerate(order)}
    queue = {"v": g.vector, "s": g.scalar, "t": g.tensor, "g": g, "y": g.sync}
    known = {q: 0 for q in queue}
    for i in order:
        o = ops[i]
        o["waits"] = []
        k = known[o["q"]]
        for j in sorted(deps[i], key=lambda j: -place[j]):
            if not k >> j & 1:
                o["waits"].append(j)
                ops[j]["inc"] = True
                k |= ops[j]["done"]
        known[o["q"]] = k
        o["seen"] = k
        o["done"] = k | 1 << i
    last = {p: [] for p in POOLS}
    for i in order:
        o = ops[i]
        e = queue[o["q"]]
        for j in reversed(o["waits"]):
            e.wait_ge(T.sem[ops[j]["sem"]], ops[j]["count"])
        for s, n in o["ext"]:
            e.wait_ge(T.sem[s], n)
        if o["fn"] is None:
            continue
        ins = o["fn"](e)
        if o["inc"]:
            pool = "d" if o["dma"] else o["q"]
            step = 16 if o["dma"] else 1
            use = last[pool]
            free = [s for s in range(len(use)) if o["seen"] >> use[s][0] & 1]
            if free:
                s = free[0]
                use[s] = (i, use[s][1] + step)
            else:
                s = len(use)
                assert s < POOLS[pool], pool
                use.append((i, step))
            o["sem"], o["count"] = "%s%d" % (pool, s), use[s][1]
            ins.then_inc(T.sem[o["sem"]], step)


def _mate(T, core, t):
    return T.cores[T.rank_of(core) ^ STEP[t]]


def _helper(T, topo, core, t):
    mate = _mate(T, core, t)
    if topo.chip(mate) == topo.chip(core):
        return None
    here = [c for c in topo.cores_of(core) if topo.die(c) == topo.die(core)]
    there = [c for c in topo.cores_of(core) if topo.die(c) != topo.die(core)]
    h = there[here.index(core)]
    return h if T.rank_of(h) is None and topo.may_write(h, mate) else None


def _hand_on(g, core, T, topo):
    sent = 0
    for t in range(R):
        for c in T.cores:
            if _helper(T, topo, c, t) == core:
                mate = _mate(T, c, t)
                rid, pid = topo.addr(mate)[:2]
                lo, hi = SEG[0]
                g.wait_ge(T.sem["hop%d" % t], 2 * len(topo.engines(c, core)))
                arr, mask = T.sem["arr%d" % (2 * t)], topo.mask(core, mate)
                g.remote_dma(T["ql%d" % t][:, lo:hi].bitcast(dt.uint8), T["qh%d" % t][:].bitcast(dt.uint8),
                             arr, T.sem.sent, pid, rid, mask)
                g.remote_dma(T["sl%d" % t][:, lo:hi], T["sh%d" % t][:], arr, T.sem.sent, pid, rid, mask)
                sent += 2 * len(topo.engines(core, mate))
    if sent:
        g.wait_ge(T.sem.sent, sent)


def rank_program(g, core, T, topo):
    rank = T.rank_of(core)
    if rank is None:
        _hand_on(g, core, T, topo)
        return
    ops = []

    def V(name, lo=0, hi=None, step=1):
        hi = SCRATCH[name][1][1] if hi is None else hi
        view = T[name][:, lo:hi] if step == 1 else T[name][:, lo:hi:step]
        return (view, [(name, lo, hi, step)], len(range(lo, hi, step)), 0.5 if SCRATCH[name][2] in (BF, U16) else 1.0)

    def BACK(name, hi, n):
        return (T[name][:, hi:hi - n:-1], [(name, hi - n + 1, hi + 1, 1)], n, 1.0)

    def X(t, lo, hi, step=1):
        at = 4 * C if t < R else 0
        return V("x%d" % t, at + lo, at + hi, step)

    def IND(win, off, words=False):
        view = win[0].bitcast(dt.uint32) if words else win[0]
        return (view.indirect(off[0]), win[1] + off[1], 16 * off[2], None)

    def P(bank, n, at=0):
        return V("ps", 512 * bank + at, 512 * bank + n)

    def op(q, fn, w=(), r=(), cost=60.0, lat=None, dma=False, after=(), behind=(), ext=()):
        wa = [a for x in w for a in x[1]]
        ra = [a for x in r if isinstance(x, tuple) for a in x[1]]
        banks = set(a[1] // 512 for a in wa + ra if a[0] == "ps")
        ops.append({"q": q, "fn": fn, "w": wa, "r": ra, "banks": banks, "dma": dma, "after": set(after),
                    "behind": set(behind), "follow": [], "ext": list(ext), "inc": False, "cost": cost,
                    "lat": cost if lat is None else lat})
        return len(ops) - 1

    def turns(calls):
        for a, b in zip(calls, calls[1:]):
            ops[b]["follow"].append(a)

    def ap(x):
        return x[0] if isinstance(x, tuple) else x

    def time(i, *more, each=None):
        if i[3] is None:
            return 55.0 + 1.6 * CYC * i[2]
        return CYC * max(64.0, i[2] * (each or max(x[3] for x in (i,) + more)))

    def copy(o, i, **more):
        return op("v", lambda e: e.tensor_copy(o[0], i[0]), [o], [i], time(i, o), **more)

    def scatter(win, off, i):
        o = IND(win, off)
        return op("v", lambda e: e.tensor_copy(o[0], i[0]), [win], [i, off], 55.0 + 3.8 * CYC * i[2])

    def tt(o, a, b, f):
        each = 1.0 if b[1][0][0] == "ps" else 2.0
        return op("v", lambda e: e.tensor_tensor(o[0], a[0], b[0], f), [o], [a, b], time(a, each=each))

    def ts(o, a, s1, f1, s2=None, f2=None):
        if f2 is None:
            return op("v", lambda e: e.tensor_scalar(o[0], a[0], ap(s1), None, f1), [o], [a, s1], time(a, o))
        return op("v", lambda e: e.tensor_scalar(o[0], a[0], ap(s1), ap(s2), f1, f2), [o], [a, s1, s2], time(a, o))

    def fold(o, i, f):
        return op("v", lambda e: e.tensor_reduce(o[0], i[0], AxisListType.X, f), [o], [i], time(i, each=1.0))

    def scan(o, d0, d1, init, f0, f1):
        return op("v", lambda e: e.tensor_tensor_scan(o[0], d0[0], d1[0], ap(init), f0, f1), [o], [d0, d1, init],
                  time(d0, d1, o))

    def turn(o, i):
        return op("v", lambda e: e.transpose(o[0], i[0]), [o], [i], time(i))

    def fill(o, c):
        return op("v", lambda e: e.memset(o[0], c), [o], [], time(o))

    def quant(n, lo, hi, i, **more):
        qq, sc = V("q" + n, lo, hi), V("s" + n, lo, hi)
        return op("v", lambda e: e.quantize_mx(qq[0], sc[0], i[0]), [qq, sc], [i], 15.0 + 0.26 * i[2], **more)

    def act(o, i, f, bias=None, scale=None, acc=None, **more):
        kw = {}
        if bias is not None:
            kw["bias"] = ap(bias)
        if scale is not None:
            kw["scale"] = ap(scale)
        if acc is not None:
            kw["accum_out"] = acc[0]
        return op("s", lambda e: e.activation(o[0], i[0], f, **kw), [o] + ([acc] if acc else []), [i, bias, scale],
                  time(i, each=1.0), **more)

    def mx(bank, sn, slo, mn, lo, hi, **more):
        o = P(bank, hi - lo)
        a, b = V("q" + sn, slo, slo + 128), V("s" + sn, slo, slo + 128)
        c, d = V("q" + mn, lo, hi), V("s" + mn, lo, hi)
        return op("t", lambda e: e.matmul_mx(o[0], a[0], b[0], c[0], d[0], True, True), [o], [a, b, c, d],
                  0.7 * (hi - lo + 16), **more)

    def iota(o, pattern, base, cm):
        cost = 130.0 + 2 * CYC * o[2]
        if SCRATCH[o[1][0][0]][2] != I32:
            return op("g", lambda e: e.iota(o[0], pattern, base, cm, allow_small_or_imprecise_dtypes=True), [o], [], cost)
        return op("g", lambda e: e.iota(o[0], pattern, base, cm), [o], [], cost)

    loaded = [0]

    def load(q, o, src, size, after=()):
        loaded[0] += size
        return op(q, lambda e: e.dma_start(o[0], src), [o], [], 60.0, LOCAL + loaded[0] / RATE, dma=True, after=after)

    stores = []

    def store(q, dst, src, i, size=0):
        stores.append(op(q, lambda e: e.dma_start(dst, src), [], [i], 60.0 + size / RATE, LOCAL + size / RATE, dma=True))

    sent = [0]

    def send(to, src, dst, sem, cast=False):
        rid, pid = topo.addr(to)[:2]
        sa, da = (src[0].bitcast(dt.uint8), dst[0].bitcast(dt.uint8)) if cast else (src[0], dst[0])
        mask, first = topo.mask(core, to), not sent[0]
        sent[0] += len(topo.engines(core, to))
        return op("g", lambda q: q.remote_dma(da, sa, T.sem[sem], T.sem.sent, pid, rid, mask), [], [src],
                  REMOTE if first else 100.0, REMOTE * (2 if cast else 1))

    shared = {t: [] for t in range(R)}

    def share(t, i):
        lo, hi = SEG[i]
        via = _helper(T, topo, core, t) if i == 0 else None
        if via is None:
            to, qd, sd, sem = _mate(T, core, t), V("ql%d" % t, lo, hi), V("sl%d" % t, lo, hi), "arr%d" % (2 * t)
        else:
            to, qd, sd, sem = via, V("qh%d" % t), V("sh%d" % t), "hop%d" % t
        shared[t].append(send(to, V("qx%d" % t, lo, hi), qd, sem, True))
        shared[t].append(send(to, V("sx%d" % t, lo, hi), sd, sem))

    def unpack(t, ends):
        mate = _mate(T, core, t)
        via = _helper(T, topo, mate, t)
        came = 4 * len(topo.engines(mate, core)) + 2 * len(topo.engines(mate if via is None else via, core))
        first = mx(0, "id", 0, "l%d" % t, 0, C, ext=[("arr%d" % (2 * t), came)], behind=shared[t])
        for b in range(1, 4):
            mx(b, "id", 128 * b, "l%d" % t, 0, C, behind=[first])
        for b in range(4):
            at = C * (2 * b + 1)
            for lo, hi in ((0, C // 2), (C // 2, C)):
                act(V("un%d" % t, at + lo, at + hi), P(b, hi, lo), ACT.Copy, behind=[ends])
                lo = max(lo, 1)
                act(BACK("un%d" % t, at - lo, hi - lo), P(b, hi, lo), ACT.Copy, behind=[ends])

    first = [load("y", V("ub"), T.u[:], 128 * 1024)]
    first += [load("y", X(0, 4 * lo, 4 * hi), T.x[:, 4 * lo:4 * hi], 128 * 1024) for lo, hi in SEG]
    wq = V("qw")
    turns(first + [load("y", (wq[0].bitcast(dt.uint8), wq[1]), T.wc[:], 128 * 2048, after=first),
                   load("y", V("sw"), T.ws[:], 128 * 512), load("y", V("vb"), T.v[:], 128 * 1024)])
    turns([iota(V("uli"), [[1, 2], [16, 8]], 0, 0), iota(V("pi", 0, 2), [[0, 2]], 0, 1),
           iota(V("row"), [[1, 16]], 0, 0), iota(V("dif"), [[1, 128]], 0, -1), iota(V("raw"), [[4, ZW]], -2, 0)])
    pn, pt, odd = V("pf", 2, 3), V("pf", 5, 6), V("pf", 9, 10)
    theta = V("cs", 10, 11)
    early = [fill(V("idb"), 0.0), copy(V("ul"), V("uli")), ts(V("pi", 2, 4), V("pi", 0, 2), 15, A.bitwise_and)]
    early += [ts(V("pi", 4 + k, 5 + k), V("pi", 0, 1), bits, A.bitwise_and) for k, bits in enumerate((31, 3, 1, 6, 8, 16))]
    early += [fill(V("mm", SW, 16 * SW, 64), -BIG), fill(V("mm", 0, SW), BIG), copy(V("pf", 2, 10), V("pi", 2, 10)),
              copy(V("oc16", 0, 3), V("pi", 2, 5))]
    turns(early)
    fill(V("kw", 2 * C, 2 * C + 1), 0.0)
    fill(V("pz", 0, 16), 0.0)
    for t in range(R):
        fill(V("x%d" % t, 0, 1), 0.0)
        fill(V("un%d" % t, 0, 8 * C, 2 * C), 0.0)
    ts(V("mask", 0, 16), V("row"), pn, A.is_gt)
    ts(V("mask", 16, 32), V("row"), pn, A.is_lt)
    ts(V("pf", 10, 11), V("pf", 6, 7), 128.0, A.mult, odd, A.add)
    ts(V("pf", 11, 12), V("pf", 7, 8), 16.0, A.mult, V("pf", 10, 11), A.add)
    ts(V("pf", 12, 13), V("pf", 8, 9), 0.125, A.mult, V("pf", 11, 12), A.add)
    ts(V("zl"), V("row", 0, 3, 2), V("pf", 12, 13), A.add)
    act(V("dif2"), V("dif"), ACT.Abs)
    for b in range(4):
        act(V("idb", 512 * b + b, 512 * (b + 1), 4), V("dif2"), ACT.Relu, bias=1.0, scale=-1.0)

    def late(*behind):
        for k in range(2):
            act(V("cs", 16 + k, 17 + k), odd, ACT.Identity, bias=4.0 * ZW * k, scale=4.0, behind=behind)
        act(V("cs", 8, 10), V("pf", 2, 4), ACT.Sign, behind=behind)
        act(theta, pn, ACT.Identity, bias=-15.5, behind=behind)
        act(V("cs", 0, 2), V("cs", 8, 10), ACT.Identity, bias=C - 1.0, scale=2.0)
        for k, (slope, base) in enumerate(((0.0, 0.0), (-764.0, 766.0), (2.0, 1.0), (-766.0, 769.0))):
            act(V("cs", 2 + k, 3 + k), V("cs", 8, 9), ACT.Identity, bias=base + C - 1.0, scale=slope)
        act(V("kw", 1, 2 * C + 2, 2), V("raw", 0, 385), ACT.Identity, bias=pt, behind=behind)

    quant("u", 0, 128, V("ub"))
    for k in range(2):
        qo, off = V("qup", K * k, K * k + K), V("ul", 8 * k, 8 * k + 8)
        copy((qo[0].bitcast(dt.uint32),) + qo[1:], IND(V("qu"), off, True))
        act(V("sup", K * k, K * k + K), IND(V("su"), off), ACT.Copy)

    def score(t, i, bank, key=0):
        mx(bank, "up", 128 * key, "x%d" % t, SEG[i][0], SEG[i][1])

    def keep(i, bank):
        lo, hi = SEG[i]
        return act(V("ss", max(lo, 1), hi), P(bank, K, max(lo, 1) - lo), ACT.Copy)

    def keys(i, bank):
        return act(V("kw", 2 * SEG[i][0], 2 * SEG[i][1], 2), P(bank, K), ACT.Copy)

    chain = [(7, V("hl", 0, 128)), (15, V("hl", 128, 192)), (15, V("hl", 192, 256)), (15, P(4, 64, 1)), (15, P(4, 128, 64))]

    def rung(k, i):
        me, data = (k + 1) * SW + sum(c[1][2] for c in chain[:i]), chain[i][1]
        n = data[2]
        scan(V("mm", me + 1, me + 1 + n), data, V("mm", me - SW, me - SW + n), V("mm", me, me + 1), A.max, A.min)

    def rate(t, i):
        share(t, i)
        if i == 0:
            score(t, 0, 4)
            score(t, 0, 5, 1)
            keep(0, 4)
            keys(0, 5)
        elif i == 1:
            score(t, 1, 6)
            score(t, 1, 7, 1)
            tt(V("hl", 0, K), V("ss", K, 2 * K), P(6, K), A.min)
            tt(V("hl", K, 2 * K), V("ss", K, 2 * K), P(6, K), A.max)
            keep(1, 6)
            keys(1, 7)
        else:
            score(t, 2, 4)
            score(t, 2, 5)
            score(t, 2, 7, 1)
            keep(2, 5)
            rated = keys(2, 7)
            for d in range(15 + len(chain)):
                for j in range(len(chain)):
                    if 0 <= d - j < chain[j][0]:
                        rung(d - j, j)
            for lo, hi in SEG:
                lo = max(4 * lo, 1)
                act(BACK("x%d" % t, 4 * C - lo, 4 * hi - lo), X(t, lo, 4 * hi), ACT.Copy, behind=[rated])
            for k in range(2):
                act(V("z", ZW * k, ZW * k + ZW), V("raw"), ACT.Identity, bias=1.0 + 3 * k, scale=0.0, behind=[rated])
            if t == 0:
                late(rated)

    def order(t):
        above, p4 = V("col", 0, 1), V("col", 1, 2)
        acc = [V("col", 2 + k, 3 + k) for k in range(2)]
        thr = V("mm", 16 * SW - 1, 16 * SW)
        n = {}
        n["top"] = act(V("top", 0, 15), V("mm", 2 * SW - 1, 16 * SW, SW), ACT.Sign, bias=thr, scale=-1.0, acc=above)
        for k, (lo, hi) in enumerate(HALF):
            body, fa, fb, cap, cnt = [V("ss", lo + 1, hi + 1)] + [V(b, lo, hi) for b in ("fa", "fb", "cap", "cnt")]
            n["fa", k] = ts(fa, body, thr, A.is_gt)
            n["fs", k] = act(V("fs", lo, hi), body, ACT.Sign, bias=thr, scale=-1.0)
            n["cap", k] = scan(cap, fa, fa, V("cap", lo - 1, lo) if k else above, A.add, A.min)
            n["fb", k] = ts(fb, V("fs", lo, hi), 0.0, A.is_le)
            n["cnt", k] = scan(cnt, fb, cap, V("cnt", lo - 1, lo) if k else -15.0, A.add, A.min)
            act(V("ft", lo, hi), cnt, ACT.Sign, bias=theta, scale=-1.0, acc=acc[k])
        turns([n["top"], n["fs", 0], n["fs", 1]])
        turns([n[k] for k in (("fa", 0), ("fa", 1), ("cap", 0), ("fb", 0), ("fb", 1), ("cap", 1), ("cnt", 0), ("cnt", 1))])
        if t == 0:
            for b in range(4):
                quant("id", K * b, K * b + K, V("idb", 4 * K * b, 4 * K * (b + 1)), behind=[n["cnt", 0]])
            quant("v", 0, 128, V("vb"), behind=[n["cnt", 1]])
        o1, o2 = "o1_%d" % t, V("o2_%d" % t)
        ts(V(o1), V("cs", 0, 6), acc[0], A.add, acc[1], A.add)
        kw = V("kw", 0, 2 * C + 2)
        copy(V("gr", 0, 32), IND(kw, V(o1, 0, 2)))
        ends = act(V("gr", 64, 96), IND(kw, V(o1, 4, 6)), ACT.Copy)
        copy(V("gr", 32, 64), IND(kw, V(o1, 2, 4)))
        unpack(t, ends)
        kh, kl, ta, tb = V("gr", 0, 16), V("gr", 33, 49), V("gr", 64, 80), V("gr", 65, 81)
        mine = IND(V("tt"), V("oc16", 2, 3))
        turns([turn(V("tt"), V("gr", 0, 32)),
               tt(V("ln"), tb, ta, A.subtract),
               tt(V("sm", 0, 16), kh, kl, A.is_lt),
               tt(V("sm", 16, 32), ta, tb, A.add),
               tt(V("cmp", 0, 16), mine, kh, A.is_lt),
               tt(V("wt"), IND(V("ln"), V("oc16", 0, 2)), V("mask"), A.mult),
               tt(V("cmp", 16, 32), mine, kh, A.is_le),
               tt(V("sm", 32, 48), V("sm", 0, 16), V("sm", 16, 32), A.mult),
               tt(V("pr"), V("cmp"), V("wt"), A.mult),
               tt(V("pz", 16, 32), ta, V("sm", 32, 48), A.subtract)])
        fold(p4, V("pr"), A.add)
        ts(o2, V("cs", 16, 18), p4, A.add, 0.25, A.mult)
        scatter(V("z"), o2, V("pz"))
        for k, (lo, hi) in enumerate(ROWS):
            n["r", k] = scan(V("wr", lo, hi), V("z", lo, hi), V("z", ZW + lo, ZW + hi),
                             V("wr", lo - 1, lo) if lo else 0.0, A.mult, A.add)
        for i, (lo, hi) in enumerate(SEG):
            for k in range(2):
                n["T", i, k] = turn(V("tz", 2 * lo + K * k, 2 * lo + K * k + K), V("wr", lo + 16 * k, hi + 16 * k))
            if i == 2:
                n["L", i] = ts(V("far%d" % t), IND(V("tz", 0, 2 * K), V("zl", 0, 1)), 0.25, A.mult, C + 0.5, A.add)
            else:
                n["L", i] = ts(V("lst%d" % t, 32 * i, 32 * i + 32), IND(V("tz", 2 * lo, 2 * hi), V("zl")),
                               4.0 * C + 2, A.add)
        return n

    def gather(i, b, o, src, **more):
        return copy(o, src, **more) if b < ONV[i] else act(o, src, ACT.Copy, **more)

    def layer(t, i, bank, n):
        (lo, hi), e = SEG[i], "e%d" % t
        n["Q", i] = quant(e, lo, hi, V(e, 4 * lo, 4 * hi))
        for b in range(4):
            mx(bank + b, "w", 128 * b, e, lo, hi)
            n["R", i, b] = act(V("rl", C * b + lo, C * b + hi), P(bank + b, K), ACT.Relu, scale=0.015625)
            n["A", i, b] = tt(X(t + 1, 4 * lo + b, 4 * hi, 4), V("rl", C * b + lo, C * b + hi),
                              V(e, 4 * lo + b, 4 * hi, 4), A.add)
        n["P", i] = quant("x%d" % (t + 1), lo, hi, X(t + 1, 4 * lo, 4 * hi))

    def finish(i):
        lo, hi = SEG[i]
        mx(4 + i, "v", 0, "x%d" % R, lo, hi)
        cq = V("qx%d" % R, lo, hi)
        store("y", T.oc[:, 4 * lo:4 * hi], cq[0].bitcast(dt.uint8), cq, 128 * 512)
        act(V("yb", lo, hi), P(4 + i, K), ACT.Copy)
        store("s" if i == 2 else "y", T.y[:, lo:hi], T.yb[:, lo:hi], V("yb", lo, hi), 128 * 512)

    for i, (lo, hi) in enumerate(SEG):
        quant("x0", lo, hi, X(0, 4 * lo, 4 * hi))
        rate(0, i)
    for t in range(R):
        last = t == R - 1
        xo, e, mate = "x%d" % t, "e%d" % t, _mate(T, core, t)
        n = order(t)
        told = send(mate, V("far%d" % t, 0, 8), V("got%d" % t), "arr%d" % (2 * t + 1))
        for i, (lo, hi) in enumerate(SEG):
            for b in range(4):
                o = V(e, 4 * lo + b, 4 * hi, 4)
                if i < 2:
                    n["G", i, b] = gather(i, b, o, IND(V(xo), V("lst%d" % t, 32 * i + 8 * b, 32 * i + 8 * b + 8)))
                else:
                    n["G", i, b] = gather(i, b, o, IND(V("un%d" % t, 2 * C * b, 2 * C * (b + 1)), V("got%d" % t)),
                                          behind=[told], ext=[("arr%d" % (2 * t + 1), len(topo.engines(mate, core)))])
        for i in range(3):
            layer(t, i, 4 * (i % 2), n)
        for names in (VEC, SCA):
            turns([n[(w[0],) + tuple(int(d) for d in w[1:])] for w in names.split()])
        if last:
            act(V("olb"), V("wr"), ACT.Abs, bias=0.5, scale=0.25, behind=[n["R", 2, 3]])
            for k in range(2):
                store("y", T.ol[k:8:2, :], T.olb[16 * k:128:32, 16 * k:16 * k + C], V("olb"))
        for i in range(3):
            if last:
                finish(i)
            else:
                rate(t + 1, i)
    for k in range(4):
        store("ys"[k // 2], T.osc[4 * k:4 * k + 4, :], T["sx%d" % R][32 * k:32 * k + 4, :], V("sx%d" % R))
    op("g", None, after=stores, ext=[("sent", sent[0])], behind=range(len(ops)))
    _emit(ops, g, T)
